import numpy as np, ml_dtypes
CORES = [66,74,82,90,194,202,210,218]
N = 8
import mx_ref
BF = ml_dtypes.bfloat16
def gentries(a):
    return np.ascontiguousarray(a.reshape(8, 16, -1).transpose(0, 2, 1)).reshape(8, -1)
def gtable(e):
    e = np.asarray(e); return np.ascontiguousarray(e.reshape(8, -1, 16).transpose(0, 2, 1)).reshape(128, -1).astype(np.int32)
def gcols(t, e):
    v = np.concatenate([t.reshape(8, 16, -1, 4), np.zeros((8, 16, 1, 4), BF)], axis=2)
    return np.ascontiguousarray(np.stack([v[g][:, e[g]] for g in range(8)])).reshape(128, -1)
def tile(rs):
    return np.stack(rs, axis=2).reshape(128, -1).astype(BF)
def pick(q, e):
    c = np.concatenate([q[0].reshape(128, -1, 4), np.zeros((128, 1, 4), np.uint8)], axis=1); s = np.concatenate([q[1], np.ones((16, 1), np.uint8)], axis=1)
    return (np.ascontiguousarray(c[:, e].reshape(128, -1)), np.ascontiguousarray(s[:, e]))
def join(*qs):
    return (np.concatenate([q[0] for q in qs], axis=1), np.concatenate([q[1] for q in qs], axis=1))
def put(q, e, v):
    c, s = q[0].reshape(128, -1, 4).copy(), q[1].copy(); c[:, e] = v[0].reshape(128, -1, 4); s[:, e] = v[1]
    return (c.reshape(128, -1), s)
def pk(c, s):
    return (np.ascontiguousarray(c), mx_ref.live(s))
def emit(q):
    return q[0], q[1]
def packed(v, rng):
    q = [mx_ref.quantize(np.ascontiguousarray(v[r])) for r in range(N)]
    return np.stack([a for a, b in q]), np.stack([mx_ref.plane(b, rng) for a, b in q])
def values_of_codes():
    e, c = np.zeros((128, 128, 4), np.float32), np.zeros((128, 2, 4), np.uint8)
    e[np.arange(128), np.arange(128), 0] = 1
    c[:127, :, 0] = np.arange(256).reshape(2, 128).T[:127]
    return mx_ref.matmul(mx_ref.quantize(e.reshape(128, 512).astype(BF)), (c.reshape(128, 8), np.full((16, 2), 127, np.uint8))).T.reshape(-1).astype(np.float64)
CODE_VALUE, SCALE_VALUE = values_of_codes(), 2.0 ** (np.arange(256) - 127.0)
def decode(q):
    return (CODE_VALUE[q[0]].reshape(16, 8, -1, 4) * SCALE_VALUE[q[1]][:, None, :, None] + 0.0).reshape(128, -1).astype(np.float32)
def f(rng, *shape):
    return mx_ref.flush((rng.standard_normal(shape, dtype=np.float32) * np.exp2(rng.integers(-2, 3, shape[:-1] + (1,)))).astype(BF))
def wide(rng, *shape, cols=0):
    v = rng.standard_normal(shape, dtype=np.float32) * np.exp2(rng.integers(-12, 13, shape)).astype(np.float32)
    if cols: v *= np.repeat(np.exp2(rng.integers(-cols, cols + 1, shape[:-2] + (1, shape[-1] // 4))) * (rng.random(shape[:-2] + (1, shape[-1] // 4)) > 0.0625), 4, axis=-1).astype(np.float32)
    return mx_ref.flush(v.astype(BF))
C, DOUBLINGS = 288, 9
STEP = [4, 1, 2]
def numbers_of(rng):
    return {"x": np.array(f(rng, N, 128, 4 * C)), "u": np.array(f(rng, N, 128, 512)), "v": np.array(f(rng, N, 128, 512))}
def links(rng, far=False):
    l = rng.permuted(np.tile(np.arange(C), (N, 8, 2, 1)), axis=3)
    if far:
        for r in range(N):
            for i, g in enumerate(rng.permutation(8)[:6]):
                o = rng.permutation(C)
                l[r, g, 0, o] = np.append(o[1:], o[[0, C - 1, C // 2][i % 3]])
                if i < 3: l[r, g, 1] = l[r, g, 0]
    return l
def stored(l):
    return {"la": np.stack([gtable(l[r, :, 0]) for r in range(N)]), "lb": np.stack([gtable(l[r, :, 1]) for r in range(N)])}
def layers(rng, still=[]):
    w = np.array(f(rng, N, 128, 2048)).reshape(N, 8, 16, 4, 8, 16, 4)
    for i in still:
        w[:, :, i] = 0
        w[:, :, :, :, :, i] = 0
    return w
def weights(rng, w):
    c, p = packed(np.ascontiguousarray(w).reshape(N, 128, 2048), rng)
    return {"wc": c, "ws": p}
def setup_inputs(rng):
    return {**numbers_of(rng), **stored(links(rng)), **weights(rng, layers(rng))}
def setup_inputs_ties(rng):
    d = numbers_of(rng)
    o = rng.permutation(N)
    k = rng.integers(-2, 3, (N, 8, C))
    k[o[1]] = -rng.integers(1, 5, (8, C))
    far = rng.permutation(8)
    k[o[2], far[:4]] = 1
    k[o[3], rng.permutation(8)[:4]] = -1
    l = links(rng, True)
    way = rng.permutation(C)
    way[-2:] = np.sort(way[-2:])
    for g, end, top in ((far[4], way[-1], way[-1]), (far[5], way[0], 0)):
        l[o[2], g, 0, way] = np.append(way[1:], end)
        l[o[2], g, 1] = np.arange(C)
        k[o[2], g] = 1
        k[o[2], g, top] = 2
    x = d["x"].reshape(N, 8, 16, C, 4)
    x[:, :, 0] = 0
    x[:, :, 0, :, 0] = k.astype(np.float32).astype(BF)
    u = d["u"].reshape(N, 128, 128, 4)
    u[:, :, ::16] = 0
    for r in range(N):
        for h in range(0, 128, 16): u[r, h, h, 0] = 0.0 if r == o[0] else 1.0
    return {"x": x.reshape(N, 128, 4 * C), "u": u.reshape(N, 128, 512), "v": d["v"], **stored(l), **weights(rng, layers(rng, [0]))}
def setup_inputs_near(rng):
    d = numbers_of(rng)
    x = d["x"].astype(np.float32).reshape(N, 8, 16, C, 4)
    x[:, :, 0] = 0
    x[:, :, 8:] = 0
    u = d["u"].reshape(N, 128, 128, 4)
    u[:, :, ::16] = 0
    w = layers(rng, [0, 8, 9, 10, 11, 12, 13, 14, 15])
    o = rng.permutation(N) % 4
    for r in range(N):
        s = rng.integers(0, 16, (8, C))
        digits = ((s[:, :, None] >> np.arange(4)) & 1) * np.exp2(np.arange(4) - 23.0)
        if o[r] < 3: x[r, :, 12, :, 0] = rng.choice([-1.0, 1.0], (8, C)) * 2.0 ** -20
        if o[r] < 2:
            x[r, :, 0, :, 0] = np.where(rng.permutation(8) < 4, -1.0, 1.0)[:, None]
            x[r, :, 8] = digits
            x[r, :, 11, :, 0] = 2.0 ** -10
        elif o[r] == 2: x[r, :, 8] = digits * rng.choice([-1.0, 1.0], (8, C, 1))
        else:
            e = rng.integers(-1, 2, (8, C)) * 2.0 ** -30
            x[r, :, 8, :, 0] = 1.25 * e
            x[r, :, 9, :, 0] = -1.125 * e
            x[r, :, 15, :, 0] = 2.0 ** -30
            for g in range(8):
                w[r, g, 12, 0, g, 10, 0] = 2.0 ** -18
                w[r, g, 14, 0, g, 10, 0] = 2.0 ** -8
        at = [0, C - 1, int(rng.integers(C)), int(rng.integers(C))]
        for g, j in zip(rng.permutation(8)[:4], at): x[r, g, 0, j, 0] = 2.0 ** 29 * rng.choice([-1.0, 1.0])
        k = 1.0 if o[r] == 0 else 2.0 ** -30
        for h in range(0, 128, 16):
            u[r, h, h, 0] = k if o[r] < 2 else 1.0
            if o[r] < 2: u[r, h + 11, h, 0] = k
            if o[r] < 3: u[r, h + 8, h] = k
            else:
                u[r, h + 8, h, 0] = k
                u[r, h + 9, h, 0] = 1.125 * k
                u[r, h + 10, h, 0] = k
    return {"x": x.reshape(N, 128, 4 * C).astype(BF), "u": u.reshape(N, 128, 512), "v": d["v"], **stored(links(rng, True)), **weights(rng, w)}
def setup_inputs_odd(rng):
    d = numbers_of(rng)
    x = (1.0 + (2 * rng.integers(0, 64, (N, 16, 8, C, 4)) + 1) * 2.0 ** -7) * np.exp2(-rng.integers(0, 7, (N, 16, 8, C, 4)).astype(np.float64)) * rng.choice([-1.0, 1.0], (N, 16, 8, C, 4))
    x[:, :, 0, :, 0] = np.where(rng.random((N, 16, C)) < 0.25, 1.875, 1.96875) * 2.0 ** 8
    x[:, ::2, 1, :, 0] = rng.choice([-1.0, 1.0], (N, 8, C)) * (8 + rng.integers(0, 2, (N, 8, C))) * 2.0 ** -8
    u = d["u"].reshape(N, 16, 8, 128, 4)
    u[:, :, :, ::16] = 0
    for g in range(8): u[:, 2 * g, 1, 16 * g, 0] = 1.0
    return {"x": x.astype(np.float32).reshape(N, 128, 4 * C).astype(BF), "u": u.reshape(N, 128, 512), "v": d["v"], **stored(links(rng)), **weights(rng, layers(rng, [0, 8]))}
def setup_inputs_ends(rng):
    d = numbers_of(rng)
    o, e = rng.permutation(N) % 4, rng.permutation(N) % 4
    m = int(rng.integers(8))
    l = links(rng, True)
    small = -(1.0 + 0.125 * rng.integers(0, 8, (N, 8, 16, C, 4)))
    x = -(0.88 + 0.08 * rng.random((N, 8, 16, C, 4))) * 2.0 ** 30
    x[o == 1] *= rng.choice([-1.0, 1.0], (N, 1, 1, C, 1))[o == 1]
    x[o == 2] = small[o == 2] * 2.0 ** -30
    x[o == 3] = d["x"].astype(np.float32).reshape(N, 8, 16, C, 4)[o == 3][:, :, :, :1]
    x[:, m] = small[:, m] * 2.0 ** -20
    u = d["u"].astype(np.float32).reshape(N, 8, 16, 128, 4)
    v = rng.choice([-1.0, 1.0], (N, 128, 512)) * np.where(o < 2, 2.0 ** 30, 2.0 ** -30)[:, None, None]
    w = np.zeros((N, 128, 4, 128, 4), np.float32)
    i = np.arange(128)
    for r in range(N):
        h = rng.permutation(8)
        c = np.where(h < 2, 0.0, h % 2 * 2.0 - 1.0)[:, None]
        if o[r] < 2: u[r, :, :, ::16] = c * (0.9 + 0.1 * rng.random((8, 16, 8, 4))) * 2.0 ** 30
        if o[r] == 2: u[r, :, :, ::16] = c * (1.0 + 0.125 * rng.integers(0, 8, (8, 16, 8, 4))) * 2.0 ** -30
        if o[r] == 3: u[r, :, :, ::16] *= np.abs(c).astype(np.float32)
        k = np.zeros(8)
        if o[r] < 2: k = rng.choice([-1.0, 1.0], 8) * np.array([0.75, 0.5, 2.0 ** -8])[rng.permutation(8) % 3]
        k[m] = 2.0 ** 8
        for b in range(4): w[r, i, b, i, b] = k[i // 16]
        if e[r] < 2:
            l[r, :, e[r]] = C - 1
            l[r, :, 1 - e[r]] = 0
        if e[r] == 2: l[r] = rng.integers(0, C, (8, 2, C))
    u[:, m, :, ::16] = 0
    return {"x": x.astype(np.float32).reshape(N, 128, 4 * C).astype(BF), "u": u.reshape(N, 128, 512).astype(BF), "v": v.astype(np.float32).astype(BF), **stored(l), **weights(rng, w.astype(BF))}
def setup_inputs_spread(rng):
    d = setup_inputs(rng)
    d["x"] = wide(rng, N, 128, 4 * C, cols=6)
    return d
def check_inputs(d):
    b = []
    for k in ("x", "u", "v"):
        a = np.abs(d[k].astype(np.float32))
        if not (np.isfinite(a).all() and ((a == 0) | (a >= 2.0 ** -30) & (a <= 2.0 ** 30)).all()): b.append("a value of " + k)
    for k in ("la", "lb"):
        if not ((d[k] >= 0) & (d[k] < C)).all(): b.append("an entry of " + k)
    none, least, most = [emit(mx_ref.quantize(np.full((128, 16), k, np.float32).astype(BF)))[1][0, 0] for k in (0.0, 2.0 ** -8, 2.0 ** 8)]
    for r in range(N):
        if ((d["wc"][r] == 0x7F) | (d["wc"][r] == 0xFF)).any(): b.append("wc: a code that is no number")
        s = mx_ref.live(d["ws"][r])
        if ((s != none) & ((s < least) | (s > most))).any(): b.append("ws: a scale out of range")
        if (((d["wc"][r].reshape(16, 8, 512, 4) & 0x7F) != 0) & (s == none)[:, None, :, None]).any(): b.append("wc: a code other than zero under the scale of zeros")
    return b
def look(t, e):
    return np.take_along_axis(t, e, axis=1)
def leaders(p):
    low, at = np.tile(np.arange(C), (8, 1)), p
    for k in range(DOUBLINGS):
        low = np.minimum(low, look(low, at))
        at = look(at, at)
    return look(low, at)
def reference(x, u, v, la, lb, wc, ws):
    qu = [mx_ref.quantize(u[r]) for r in range(N)]
    lay = [pk(wc[r], ws[r]) for r in range(N)]
    l0, l1 = [gentries(la[r]) for r in range(N)], [gentries(lb[r]) for r in range(N)]
    now = [x[r] for r in range(N)]
    for step in STEP:
        own, torn, sent = [], [], []
        for r in range(N):
            q = mx_ref.quantize(now[r])
            s = mx_ref.matmul(qu[r], q)[::16] + np.float32(0.0)
            p = np.where(s < 0, l1[r], l0[r])
            lead = leaders(p)
            e = np.where(lead == np.arange(C), lead, p)
            own.append(decode(q).astype(BF))
            torn.append(e)
            z = own[r]
            for k in range(3):
                z = ((z.astype(np.float32) + gcols(z, e).astype(np.float32)) * np.float32(0.5)).astype(BF)
                e = look(e, e)
            sent.append(mx_ref.quantize(z))
            change = look(s, lead) > s
            l0[r], l1[r] = np.where(change, l1[r], l0[r]), np.where(change, l0[r], l1[r])
        for r in range(N):
            z = sent[(r - step) % N]
            h = tile([mx_ref.matmul(pick(lay[r], np.arange(128 * b, 128 * b + 128)), z) * np.float32(0.03125) for b in range(4)])
            now[r] = (own[r].astype(np.float32) + gcols(h, torn[r]).astype(np.float32)).astype(BF)
    y, ls = np.zeros((N, 128, C), np.float32), np.zeros((N, 8, 2 * C), np.float32)
    oc, osc = np.zeros((N, 128, 4 * C), np.uint8), np.zeros((N, 16, C), np.uint8)
    for r in range(N):
        q = mx_ref.quantize(now[r])
        y[r] = mx_ref.matmul(mx_ref.quantize(v[r]), q)
        ls[r] = np.concatenate([l0[r], l1[r]], axis=1)
        oc[r], osc[r] = emit(q)
    return {"y": y, "ls": ls, "oc": oc, "osc": osc}

@@ -1,0 +1,408 @@
+from concourse.mybir import dt, AluOpType, ActivationFunctionType
+
+C = 288
+K = C // 16
+STEP = [4, 1, 2]
+ROUNDS = len(STEP)
+HALF = C // 2
+
+SCRATCH = {}
+
+
+def _declare():
+    s = SCRATCH
+    for k in range(ROUNDS + 1):
+        s["xt%d" % k] = ("sbuf", [128, 4 * C], "bfloat16")
+        s["xq%d" % k] = ("sbuf", [128, C], "float8_e4m3fn_x4")
+        s["xs%d" % k] = ("sbuf", [128, C], "uint8")
+    for k in range(ROUNDS):
+        s["aq%d" % k] = ("sbuf", [128, C], "float8_e4m3fn_x4")
+        s["as%d" % k] = ("sbuf", [128, C], "uint8")
+        for n in ("ta", "tb", "td"):
+            s[n + str(k)] = ("sbuf", [128, 32], "uint16")
+        s["zq%d" % k] = ("sbuf", [128, C], "float8_e4m3fn_x4")
+        s["zs%d" % k] = ("sbuf", [128, C], "uint8")
+    for n, w in (("ut", 512), ("vt", 512), ("em", 520), ("en", 520), ("e1", 520), ("e8", 520), ("ic", C), ("im", C), ("m1", C), ("mk", C),
+                 ("dw", C), ("bb", C), ("sa", C), ("sb", C), ("fl", C), ("cm", C), ("rb", C), ("rc", C), ("rd", C),
+                 ("q0", C), ("q1", C), ("q2", C), ("xg", C), ("alt", 2 * C), ("st", 12 * C), ("tab", 24 * C), ("ic2", C), ("zd", 6 * C),
+                 ("fo", 4 * C), ("z0", 4 * C), ("z1", 4 * C), ("z2", 4 * C), ("z3", 4 * C), ("gb", 2 * C), ("hb", 4 * C)):
+        s[n] = ("sbuf", [128, w], "bfloat16")
+    for n, w in (("ol", 32 * 9), ("snt", 32 * 3 * ROUNDS), ("uo", 32)):
+        s[n] = ("sbuf", [128, w], "uint16")
+    s["lo"] = ("sbuf", [128, 64], "uint16")
+    for n, w in (("ri", C), ("rr", C), ("pi", 8), ("pj", 8), ("k16", 24), ("uj", 8), ("la32", 24), ("lb32", 24)):
+        s[n] = ("sbuf", [128, w], "int32")
+    for n, w in (("wa", C), ("ssb", C), ("ssc", C), ("fi", C), ("lrep", 2 * C), ("yo", C), ("sc0", 8), ("sc1", 8), ("pf", 8), ("cw", 24), ("tm", 24), ("pw", 24),
+                 ("cp", 24), ("tn", 24), ("tw", 24), ("xm", 24), ("xd", 24), ("xe", 24), ("l1f", 24), ("lst", 32 * 8)):
+        s[n] = ("sbuf", [128, w], "float32")
+    for n, w in (("uq", 128), ("uq2", 128), ("vq", 128), ("wq", 512), ("c1", 512), ("c8", 512)):
+        s[n] = ("sbuf", [128, w], "float8_e4m3fn_x4")
+        s[n + "s"] = ("sbuf", [128, w], "uint8")
+    for i in range(8):
+        s["ps%d" % i] = ("psum", [128, 512], "float32")
+
+
+_declare()
+SEMAPHORES = (["eV", "eA", "eP", "eG", "lsem"] + ["dx", "du", "dla", "dlb", "dwc", "dws", "dv", "dls", "doc", "dy0", "dy1"] + ["dsc%d" % i for i in range(4)]
+              + ["%s%d" % (n, k) for n in ("rx", "ra", "rb", "rd") for k in range(ROUNDS)])
+
+
+def rank_program(g, core, T, topo):
+    rank = T.rank_of(core)
+    if rank is None:
+        return
+    Q = {"V": g.vector, "A": g.scalar, "P": g.tensor, "G": g, "Y": g.sync}
+    count, known, snap, lastw, readers, total = {}, {q: {} for q in Q}, {}, {}, {}, {}
+
+    def wait_for(q, toks):
+        best = {}
+        for s, n in toks:
+            best[s] = max(n, best.get(s, 0))
+        todo = [(s, n) for s, n in best.items() if known[q].get(s, 0) < n]
+        todo = [t for t in todo if not any(u != t and snap.get(u, {}).get(t[0], 0) >= t[1] for u in todo)]
+        for s, n in todo:
+            Q[q].wait_ge(T.sem[s], n)
+            for a, b in list(snap.get((s, n), {}).items()) + [(s, n)]:
+                known[q][a] = max(b, known[q].get(a, 0))
+
+    def before(q, reads, writes):
+        toks = []
+        for b in reads:
+            if b in lastw:
+                toks.append(lastw[b])
+            if b[:2] == "ps":
+                toks += [t for t in readers.get(b, []) if t[0] != "e" + q]
+        for b in writes:
+            if b in lastw:
+                toks.append(lastw[b])
+            toks += readers.get(b, [])
+        wait_for(q, toks)
+
+    def after(q, tok, reads, writes):
+        snap[tok] = dict(known[q])
+        for b in reads:
+            readers.setdefault(b, []).append(tok)
+        for b in writes:
+            lastw[b] = tok
+            readers[b] = []
+
+    def op(q, reads, writes, call):
+        before(q, reads, writes)
+        s = "e" + q
+        count[s] = count.get(s, 0) + 1
+        call().then_inc(T.sem[s], 1)
+        total[s] = count[s]
+        after(q, (s, count[s]), reads, writes)
+
+    def dma(q, sem, reads, writes, out, in_):
+        before(q, reads, writes)
+        Q[q].dma_start(out, in_).then_inc(T.sem[sem], 16)
+        total[sem] = 16
+        after(q, (sem, 16), reads, writes)
+
+    def send(dst, sem, reads, out, in_):
+        before("G", reads, [])
+        rid, pid = topo.addr(dst, core)
+        g.remote_dma(out, in_, T.sem[sem], T.sem.lsem, pid, rid, topo.mask(core, dst))
+        total["lsem"] = total.get("lsem", 0) + len(topo.engines(core, dst))
+
+    def lands(src, sem, buf, writes=1):
+        n = writes * len(topo.engines(src, core))
+        total[sem] = n
+        for b in buf:
+            lastw[b] = (sem, n)
+            readers[b] = []
+
+    V, A, P = g.vector, g.scalar, g.tensor
+    mult, add, sub, lt, gt, eq, amin = (AluOpType.mult, AluOpType.add, AluOpType.subtract, AluOpType.is_lt, AluOpType.is_gt, AluOpType.is_equal, AluOpType.min)
+    copy = ActivationFunctionType.Copy
+    tables = {n: i * C for i, n in enumerate(["t%d" % i for i in range(9)] + ["l%d" % i for i in range(9)] + ["k%d" % i for i in range(1, 7)])}
+    lists = {n: i * 32 for i, n in enumerate(["lz%d" % i for i in range(ROUNDS + 1)] + ["dz%d" % i for i in range(ROUNDS + 1)])}
+
+    def full(n):
+        if n in tables:
+            return T.tab[:, tables[n]:tables[n] + C]
+        return T[n][:, 0:C]
+
+    picks = {n: i * 32 for i, n in enumerate(["o%d" % i for i in range(7)] + ["orr", "te"])}
+    sent = {n + str(i): (3 * i + j) * 32 for i in range(ROUNDS) for j, n in enumerate(["pt", "pu", "pv"])}
+
+    def off(n):
+        if n in picks:
+            return T.ol[:, picks[n]:picks[n] + K]
+        if n in sent:
+            return T.snt[:, sent[n]:sent[n] + K]
+        if n in lists:
+            return T.lst[:, lists[n]:lists[n] + K]
+        return T[n][:, 0:K]
+
+    def pl(n, b):
+        return T[n][:, b * C:(b + 1) * C]
+
+    def el(n, b):
+        return T[n][:, b:4 * C:4]
+
+    def ends(n):
+        return T[n][:, 15:C:16]
+
+    def bank(i, w=C):
+        return T["ps%d" % i][:, 0:w]
+
+    def vtt(out, ok, a, ak, b, bk, o):
+        op("V", ak + bk, ok, lambda: V.tensor_tensor(out, a, b, o))
+
+    def vts(out, a, s1, s2, o1, *o2, w=off, extra=()):
+        op("V", [a] + list(extra), [out], lambda: V.tensor_scalar(w(out), w(a), s1, s2, o1, *o2))
+
+    def scan(d0, d1, out):
+        op("V", [d0, d1], [out], lambda: V.tensor_tensor_scan(full(out), full(d0), full(d1), 0.0, mult, add))
+
+    def offsets(sc, out):
+        op("V", [sc, "sc1"], [out], lambda: V.tensor_scalar(off(out), ends(sc), T.sc1[:, 0:1], 144.25, mult, add))
+
+    def acopy(out, ok, in_, ik, scale=1.0):
+        op("A", ik, ok, lambda: A.activation(out, in_, copy, scale=scale))
+
+    def agather(win, o, out):
+        acopy(full(out), [out], full(win).indirect(off(o)), [win, o])
+
+    def vgather(win, o, out):
+        op("V", [win, o], [out], lambda: V.tensor_copy(full(out), full(win).indirect(off(o))))
+
+    def low(win, o, other, out):
+        vtt(full(out), [out], full(win).indirect(off(o)), [win, o], full(other), [other], amin)
+
+    def again(src, out):
+        op("V", [src], [out], lambda: V.tensor_copy(full(out), full(src)))
+
+    def tiny(out, a, b, o):
+        vtt(off(out), [out], off(a), [a], off(b), [b], o)
+
+    def quant(t, tk, q, s, w=C):
+        op("V", tk, [q], lambda: V.quantize_mx(T[q][:, 0:w], T[s][:, 0:w], T[t][:, 0:4 * w]))
+
+    def units(e, c):
+        for b in range(4):
+            op("V", [e], [c + str(b)], lambda: V.quantize_mx(T[c][:, 128 * b:128 * b + 128], T[c + "s"][:, 128 * b:128 * b + 128],
+                                                             T[e][:, 4 - b:4 - b + 512]))
+
+    def mm(i, l, a, lk, r, rs, rk, c0=0, c1=C):
+        op("P", lk + rk, ["ps%d" % i], lambda: P.matmul_mx(bank(i, c1 - c0), T[l][:, a:a + 128], T[l + "s"][:, a:a + 128],
+                                                           T[r][:, c0:c1], T[rs][:, c0:c1], True, True))
+
+    def iota(out, ok, pattern, base, cm):
+        op("G", [], [ok], lambda: g.iota(out, pattern, base, cm, allow_small_or_imprecise_dtypes=True))
+
+    dma("Y", "dx", [], ["xt0"], T.xt0[:], T.x[:])
+    dma("A", "du", [], ["ut"], T.ut[:], T.u[:])
+    dma("Y", "dla", [], ["la32"], off("la32"), T.la[:])
+    dma("A", "dlb", [], ["lb32"], off("lb32"), T.lb[:])
+    op("V", [], ["em"], lambda: V.memset(T.em[:], 0.125))
+    op("V", [], ["en"], lambda: V.memset(T.en[:], 1.0))
+    iota(T.ri[:], "ri", [[-1, C]], C, 1)
+    iota(T.pi[:, 0:1], "pi", [[0, 1]], 0, 1)
+    iota(T.uj[:, 0:8], "uj", [[16, 8]], 0, 0)
+    iota(off("k16"), "k16", [[16, K]], 0, 0)
+    op("G", ["em"], ["e8"], lambda: g.affine_select(T.e8[:], T.em[:], [[1, 520]], eq, 0.0, -4, -4))
+    iota(T.ic[:], "ic", [[1, C]], -HALF, 0)
+    op("G", ["en"], ["e1"], lambda: g.affine_select(T.e1[:], T.en[:], [[1, 520]], eq, 0.0, -4, -4))
+    iota(T.ic2[:], "ic2", [[1, C]], -HALF, 0)
+    iota(T.alt[:], "alt", [[0, C], [1, 2]], 0, 0)
+    iota(T.fi[:], "fi", [[1, C]], 0, 0)
+
+    vts("rr", "ri", 15, None, AluOpType.bitwise_and, w=full)
+    vts("m1", "rr", 1.0, None, amin, w=full)
+    vts("wa", "rr", 15.0, 65535.0, eq, mult, w=full)
+    op("V", ["pi"], ["pj"], lambda: V.tensor_scalar(T.pj[:, 0:1], T.pi[:, 0:1], 15, None, AluOpType.bitwise_and))
+    vts("mk", "m1", -1e29, None, mult, w=full)
+    vtt(full("dw"), ["dw"], full("wa"), ["wa"], full("m1"), ["m1"], add)
+    op("V", ["pj"], ["sc0"], lambda: V.tensor_scalar(T.sc0[:, 0:1], T.pj[:, 0:1], 15.0, 1.0 - 2.0 ** -16, eq, mult))
+    op("V", ["pj"], ["pf"], lambda: V.tensor_copy(T.pf[:, 0:1], T.pj[:, 0:1]))
+    op("V", ["uj"], ["uo"], lambda: V.tensor_copy(T.uo[:, 0:8], T.uj[:, 0:8]))
+    op("V", ["sc0"], ["sc1"], lambda: V.tensor_scalar(T.sc1[:, 0:1], T.sc0[:, 0:1], 2.0 ** -16, None, add))
+    vts("cw", "k16", T.pf[:, 0:1], None, add, extra=["pf"])
+    quant("ut", ["ut"], "uq", "uqs", 128)
+    op("V", ["uq", "uo"], ["uq2c"], lambda: V.tensor_copy(T.uq2[:, 0:128].bitcast(dt.uint32), T.uq[:, 0:128].bitcast(dt.uint32).indirect(T.uo[:, 0:8])))
+    op("A", ["uq", "uo"], ["uq2p"], lambda: A.activation(T.uq2s[:, 0:128], T.uqs[:, 0:128].indirect(T.uo[:, 0:8]), copy))
+    vtt(full("im"), ["im"], full("ic"), ["ic"], full("mk"), ["mk"], sub)
+    op("V", ["la32"], ["lz0"], lambda: V.tensor_copy(off("lz0"), off("la32")))
+    tiny("dz0", "lb32", "la32", sub)
+    units("e8", "c8")
+
+    for k in range(ROUNDS):
+        dst, src = T.cores[(rank + STEP[k]) % 8], T.cores[(rank - STEP[k]) % 8]
+        xt, xq, xs, aq, asc, zq, zs, lz, dz = [n + str(k) for n in ("xt", "xq", "xs", "aq", "as", "zq", "zs", "lz", "dz")]
+        ta, tb, td, pt, pu, pv = [n + str(k) for n in ("ta", "tb", "td", "pt", "pu", "pv")]
+        nx, lz1, dz1 = [n + str(k + 1) for n in ("xt", "lz", "dz")]
+        last = k == ROUNDS - 1
+        lands(src, "rx%d" % k, [aq], 2)
+        lands(src, "ra%d" % k, [ta])
+        lands(src, "rb%d" % k, [tb])
+        lands(src, "rd%d" % k, [td])
+
+        quant(xt, [xt], xq, xs)
+        mm(4, "uq2", 0, ["uq2c", "uq2p"], xq, xs, [xq])
+        send(dst, "rx%d" % k, [xq], full(aq).bitcast(dt.uint8), full(xq).bitcast(dt.uint8))
+        send(dst, "rx%d" % k, [xq], full(asc), full(xs))
+        if k == 0:
+            units("e1", "c1")
+        for b in range(4):
+            mm(b, "c1", 128 * b, ["c1%d" % b], xq, xs, [xq])
+        if k == 0:
+            wait_for("Y", [("dx", 16)])
+            dma("Y", "dwc", [], ["wqc"], T.wq[:].bitcast(dt.uint8), T.wc[:])
+            dma("Y", "dws", [], ["wqp"], T.wqs[:], T.ws[:])
+            dma("Y", "dv", [], ["vt"], T.vt[:], T.v[:])
+
+        vtt(full("bb"), ["bb"], bank(4), ["ps4"], full("mk"), ["mk"], lt)
+        scan("m1", "bb", "sa")
+        vtt(off("tm"), ["tm"], ends("sa"), ["sa"], off(dz), [dz], mult)
+        tiny("pw", "tm", lz, add)
+        op("V", ["pw"], ["o0"], lambda: V.tensor_copy(off("o0"), off("pw")))
+        acopy(full("ssb"), ["ssb"], bank(4), ["ps4"])
+
+        agather("ic", "o0", "t0")
+        agather("t0", "o0", "t1")
+        agather("t1", "o0", "t2")
+        low("ic", "o0", "ic2", "l0")
+        low("l0", "o0", "ic", "l1")
+        tiny("cp", "cw", "pw", sub)
+        op("V", ["ps4"], ["ssc"], lambda: V.tensor_copy(full("ssc"), bank(4)))
+        for j in range(1, 7):
+            sn = "sa" if j % 2 else "sb"
+            scan("dw", "t%d" % (j + 1), sn)
+            offsets(sn, "o%d" % j)
+            if j < 6:
+                agather("t%d" % (j + 1), "o%d" % j, "t%d" % (j + 2))
+            again("l%d" % j, "k%d" % j)
+            low("l%d" % j, "o%d" % j, "k%d" % j, "l%d" % (j + 1))
+        low("l7", "o6", "k6", "l8")
+
+        for b in range(4):
+            mm(4 + b, "c8", 128 * b, ["c8%d" % b], aq, asc, [aq])
+        for b in range(3):
+            acopy(pl("z0", b), ["z0%d" % b], bank(4 + b), ["ps%d" % (4 + b)])
+
+        vtt(full("fl"), ["fl"], full("l8").indirect(off("o0")), ["l8", "o0"], full("im"), ["im"], eq)
+        scan("m1", "fl", "sa")
+        vtt(off("tn"), ["tn"], ends("sa"), ["sa"], off("cp"), ["cp"], mult)
+        tiny("tw", "tn", "pw", add)
+        op("V", ["tw"], [pt], lambda: V.tensor_copy(off(pt), off("tw")))
+        send(dst, "ra%d" % k, [pt], off(ta), off(pt))
+        agather("l8", "o6", "rb")
+        acopy(pl("z0", 3), ["z03"], bank(7), ["ps7"])
+
+        def vcast0(b):
+            op("V", ["ps%d" % (4 + b)], ["d0%d" % b], lambda: V.tensor_copy(pl("zd", b), bank(4 + b)))
+
+        agather("ic", pt, "q0")
+        agather("q0", pt, "q1")
+        vgather("rb", "o6", "rc")
+        vgather("rc", "o6", "rd")
+        vcast0(0)
+        scan("dw", "q1", "sb")
+        offsets("sb", pu)
+        send(dst, "rb%d" % k, [pu], off(tb), off(pu))
+        vcast0(1)
+        agather("q1", pu, "q2")
+        scan("dw", "rd", "sa")
+        offsets("sa", "orr")
+        vtt(full("cm"), ["cm"], full("ssb").indirect(off("orr")), ["ssb", "orr"], full("ssc"), ["ssc"], gt)
+        scan("dw", "q2", "sb")
+        offsets("sb", pv)
+        send(dst, "rd%d" % k, [pv], off(td), off(pv))
+        scan("dw", "cm", "sa")
+
+        def step(i, b, o):
+            x, out = "z%d" % (i - 1), (el("z3", b) if i == 3 else pl("z%d" % i, b))
+            n = 2 * (i - 1) + b
+            vtt(out, ["z%d%d" % (i, b)], pl(x, b).indirect(off(o)), [x + str(b), o], pl("zd", n), ["d%d%d" % (i - 1, b)], add)
+
+        def twin(i, b):
+            n = 2 * i + b
+            op("V", ["z%d%d" % (i, b)], ["d%d%d" % (i, b)], lambda: V.tensor_copy(pl("zd", n), pl("z%d" % i, b)))
+
+        def stream(i, b):
+            n = {1: 0, 2: 4, 3: 8}[i] + 2 * (b - 2)
+            return n * C, (n + 2) * C
+
+        def stage(i, b, o):
+            a, e = stream(i, b)
+            s, z = stream(1, b)
+            win, one, xk = (T.st[:, s:z], T.st[:, s + 1:z:2], "u%d" % b) if i == 3 else (pl("z1", b), pl("z1", b), "z1%d" % b)
+            acopy(T.st[:, a + 1:e:2], ["y%d%d" % (i, b)], one, [xk])
+            acopy(T.st[:, a:e:2], ["w%d%d" % (i, b)], win.indirect(off(o)), [xk, o])
+
+        def pairs(i, b):
+            a, e = stream(i, b)
+            s, z = stream(1, b)
+            out, ok = (T.z3[:, b - 2:4 * C:2], ["z3%d" % b, "z3%d" % (b - 2)]) if i == 3 else (T.st[:, s:z], ["u%d" % b])
+            op("V", ["alt", "y%d%d" % (i, b), "w%d%d" % (i, b)], ok, lambda: V.tensor_tensor_scan(out, T.alt[:], T.st[:, a:e], 0.0, mult, add))
+
+        def half(b):
+            vtt(pl("z1", b), ["z1%d" % b], pl("gb", b - 2), ["gb%d" % b], bank(4 + b), ["ps%d" % (4 + b)], add)
+
+        for b in (2, 3):
+            acopy(pl("gb", b - 2), ["gb%d" % b], pl("z0", b).indirect(off(ta)), ["z0%d" % b, ta])
+        step(1, 0, ta)
+        twin(1, 0)
+        half(2)
+        stage(2, 2, tb)
+        step(1, 1, ta)
+        twin(1, 1)
+        half(3)
+        stage(2, 3, tb)
+        step(2, 0, tb)
+        twin(2, 0)
+        pairs(2, 2)
+        op("V", [td], ["te"], lambda: V.tensor_scalar(off("te"), off(td), 2.0, 1.0, mult, add))
+        stage(3, 2, "te")
+        step(2, 1, tb)
+        twin(2, 1)
+        pairs(2, 3)
+        stage(3, 3, "te")
+        for b in range(3):
+            acopy(pl("fo", b), ["fo%d" % b], bank(b), ["ps%d" % b])
+        pairs(3, 2)
+        step(3, 0, td)
+        pairs(3, 3)
+        step(3, 1, td)
+        quant("z3", ["z30", "z31", "z32", "z33"], zq, zs)
+
+        if k == 0:
+            quant("vt", ["vt"], "vq", "vqs", 128)
+        op("V", ["sa", "sc1"], ["xm"], lambda: V.tensor_scalar(off("xm"), ends("sa"), T.sc1[:, 0:1], 0.5, mult, gt))
+        tiny("xd", "xm", dz, mult)
+        vts("xe", "xm", -2.0, 1.0, mult, add)
+        tiny(lz1, lz, "xd", add)
+        tiny(dz1, dz, "xe", mult)
+        if last:
+            tiny("l1f", lz1, dz1, add)
+            op("V", [lz1], ["loa"], lambda: V.tensor_copy(T.lo[:, 0:K], off(lz1)))
+            op("V", ["l1f"], ["lob"], lambda: V.tensor_copy(T.lo[:, K:2 * K], off("l1f")))
+
+        for b in range(4):
+            mm(4 + b, "wq", 128 * b, ["wqc", "wqp"], zq, zs, [zq])
+        for b in range(4):
+            acopy(pl("hb", b), ["hb%d" % b], bank(4 + b), ["ps%d" % (4 + b)], 0.03125)
+        acopy(full("xg"), ["xg"], pl("hb", 3).indirect(off(pt)), ["hb3", pt])
+        for b in range(3):
+            vtt(el(nx, b), [nx], pl("hb", b).indirect(off(pt)), ["hb%d" % b, pt], pl("fo", b), ["fo%d" % b], add)
+        vtt(el(nx, 3), [nx], full("xg"), ["xg"], bank(3), ["ps3"], add)
+
+    acopy(T.lrep[:], ["lrep"], full("fi").indirect(T.lo[:, 0:2 * K]), ["fi", "loa", "lob"])
+    dma("Y", "dls", ["lrep"], [], T.ls[:], T.lrep[0:128:16, :])
+    xq, xs = "xq%d" % ROUNDS, "xs%d" % ROUNDS
+    quant("xt%d" % ROUNDS, ["xt%d" % ROUNDS], xq, xs)
+    mm(0, "vq", 0, ["vq"], xq, xs, [xq], 0, HALF)
+    mm(1, "vq", 0, ["vq"], xq, xs, [xq], HALF, C)
+    dma("Y", "doc", [xq], [], T.oc[:], full(xq).bitcast(dt.uint8))
+    for i in range(4):
+        dma("Y", "dsc%d" % i, [xq], [], T.osc[4 * i:4 * i + 4, :], T[xs][32 * i:32 * i + 4, :])
+    acopy(T.yo[:, 0:HALF], ["yo0"], bank(0, HALF), ["ps0"])
+    op("V", ["ps1"], ["yo1"], lambda: V.tensor_copy(T.yo[:, HALF:C], bank(1, HALF)))
+    dma("A", "dy0", ["yo0"], [], T.y[:, 0:HALF], T.yo[:, 0:HALF])
+    dma("Y", "dy1", ["yo1"], [], T.y[:, HALF:C], T.yo[:, HALF:C])
+    for s in total:
+        if known["Y"].get(s, 0) < total[s]:
+            Q["Y"].wait_ge(T.sem[s], total[s])

@@ -22,7 +22,7 @@ def _declare():
             s[n + str(k)] = ("sbuf", [128, 32], "uint16")
         s["zq%d" % k] = ("sbuf", [128, C], "float8_e4m3fn_x4")
         s["zs%d" % k] = ("sbuf", [128, C], "uint8")
-    for n, w in (("ut", 512), ("vt", 512), ("em", 520), ("en", 520), ("e1", 520), ("e8", 520), ("ic", C), ("im", C), ("m1", C), ("mk", C),
+    for n, w in (("ut", 512), ("vt", 512), ("em", 520), ("en", 520), ("e1", 520), ("e8", 520), ("ic", C), ("m1", C), ("mk", C),
                  ("dw", C), ("bb", C), ("sa", C), ("sb", C), ("fl", C), ("cm", C), ("rb", C), ("rc", C), ("rd", C),
                  ("q0", C), ("q1", C), ("q2", C), ("xg", C), ("alt", 2 * C), ("st", 12 * C), ("tab", 24 * C), ("ic2", C), ("zd", 6 * C),
                  ("fo", 4 * C), ("z0", 4 * C), ("z1", 4 * C), ("z2", 4 * C), ("z3", 4 * C), ("gb", 2 * C), ("hb", 4 * C)):
@@ -33,7 +33,7 @@ def _declare():
     for n, w in (("ri", C), ("rr", C), ("pi", 8), ("pj", 8), ("k16", 24), ("uj", 8), ("la32", 24), ("lb32", 24)):
         s[n] = ("sbuf", [128, w], "int32")
     for n, w in (("wa", C), ("ssb", C), ("ssc", C), ("fi", C), ("lrep", 2 * C), ("yo", C), ("sc0", 8), ("sc1", 8), ("pf", 8), ("cw", 24), ("tm", 24), ("pw", 24),
-                 ("cp", 24), ("tn", 24), ("tw", 24), ("xm", 24), ("xd", 24), ("xe", 24), ("l1f", 24), ("lst", 32 * 8)):
+                 ("cp", 24), ("cs", 24), ("pq", 24), ("tn", 24), ("tw", 24), ("xm", 24), ("xd", 24), ("xe", 24), ("l1f", 24), ("lst", 32 * 8)):
         s[n] = ("sbuf", [128, w], "float32")
     for n, w in (("uq", 128), ("uq2", 128), ("vq", 128), ("wq", 512), ("c1", 512), ("c8", 512)):
         s[n] = ("sbuf", [128, w], "float8_e4m3fn_x4")
@@ -181,8 +181,17 @@ def rank_program(g, core, T, topo):
     def quant(t, tk, q, s, w=C):
         op("V", tk, [q], lambda: V.quantize_mx(T[q][:, 0:w], T[s][:, 0:w], T[t][:, 0:4 * w]))
 
-    def units(e, c):
-        for b in range(4):
+    halves = ((0, HALF), (HALF, C))
+
+    def parts(n):
+        return [n + "a", n + "b"]
+
+    def quant_half(t, tk, q, s, h):
+        a, e = halves[h]
+        op("V", tk, [parts(q)[h]], lambda: V.quantize_mx(T[q][:, a:e], T[s][:, a:e], T[t][:, 4 * a:4 * e]))
+
+    def units(e, c, which=range(4)):
+        for b in which:
             op("V", [e], [c + str(b)], lambda: V.quantize_mx(T[c][:, 128 * b:128 * b + 128], T[c + "s"][:, 128 * b:128 * b + 128],
                                                              T[e][:, 4 - b:4 - b + 512]))
 
@@ -205,10 +214,7 @@ def rank_program(g, core, T, topo):
     iota(off("k16"), "k16", [[16, K]], 0, 0)
     op("G", ["em"], ["e8"], lambda: g.affine_select(T.e8[:], T.em[:], [[1, 520]], eq, 0.0, -4, -4))
     iota(T.ic[:], "ic", [[1, C]], -HALF, 0)
-    op("G", ["en"], ["e1"], lambda: g.affine_select(T.e1[:], T.en[:], [[1, 520]], eq, 0.0, -4, -4))
     iota(T.ic2[:], "ic2", [[1, C]], -HALF, 0)
-    iota(T.alt[:], "alt", [[0, C], [1, 2]], 0, 0)
-    iota(T.fi[:], "fi", [[1, C]], 0, 0)
 
     vts("rr", "ri", 15, None, AluOpType.bitwise_and, w=full)
     vts("m1", "rr", 1.0, None, amin, w=full)
@@ -224,10 +230,8 @@ def rank_program(g, core, T, topo):
     quant("ut", ["ut"], "uq", "uqs", 128)
     op("V", ["uq", "uo"], ["uq2c"], lambda: V.tensor_copy(T.uq2[:, 0:128].bitcast(dt.uint32), T.uq[:, 0:128].bitcast(dt.uint32).indirect(T.uo[:, 0:8])))
     op("A", ["uq", "uo"], ["uq2p"], lambda: A.activation(T.uq2s[:, 0:128], T.uqs[:, 0:128].indirect(T.uo[:, 0:8]), copy))
-    vtt(full("im"), ["im"], full("ic"), ["ic"], full("mk"), ["mk"], sub)
     op("V", ["la32"], ["lz0"], lambda: V.tensor_copy(off("lz0"), off("la32")))
     tiny("dz0", "lb32", "la32", sub)
-    units("e8", "c8")
 
     for k in range(ROUNDS):
         dst, src = T.cores[(rank + STEP[k]) % 8], T.cores[(rank - STEP[k]) % 8]
@@ -240,26 +244,37 @@ def rank_program(g, core, T, topo):
         lands(src, "rb%d" % k, [tb])
         lands(src, "rd%d" % k, [td])
 
-        quant(xt, [xt], xq, xs)
-        mm(4, "uq2", 0, ["uq2c", "uq2p"], xq, xs, [xq])
-        send(dst, "rx%d" % k, [xq], full(aq).bitcast(dt.uint8), full(xq).bitcast(dt.uint8))
-        send(dst, "rx%d" % k, [xq], full(asc), full(xs))
-        if k == 0:
-            units("e1", "c1")
-        for b in range(4):
-            mm(b, "c1", 128 * b, ["c1%d" % b], xq, xs, [xq])
+        xk = parts(xq)
+
+        def own():
+            for b in range(4):
+                mm(b, "c1", 128 * b, ["c1%d" % b], xq, xs, xk)
+
+        for h in (0, 1):
+            quant_half(xt, [xt] + [xt + "_%d" % b for b in range(4)], xq, xs, h)
+            mm(4 + h, "uq2", 0, ["uq2c", "uq2p"], xq, xs, [xk[h]], *halves[h])
+        send(dst, "rx%d" % k, xk, full(aq).bitcast(dt.uint8), full(xq).bitcast(dt.uint8))
+        send(dst, "rx%d" % k, xk, full(asc), full(xs))
+        if k:
+            own()
+        else:
+            op("G", ["en"], ["e1"], lambda: g.affine_select(T.e1[:], T.en[:], [[1, 520]], eq, 0.0, -4, -4))
+            iota(T.alt[:], "alt", [[0, C], [1, 2]], 0, 0)
+            iota(T.fi[:], "fi", [[1, C]], 0, 0)
         if k == 0:
             wait_for("Y", [("dx", 16)])
             dma("Y", "dwc", [], ["wqc"], T.wq[:].bitcast(dt.uint8), T.wc[:])
             dma("Y", "dws", [], ["wqp"], T.wqs[:], T.ws[:])
             dma("Y", "dv", [], ["vt"], T.vt[:], T.v[:])
 
-        vtt(full("bb"), ["bb"], bank(4), ["ps4"], full("mk"), ["mk"], lt)
-        scan("m1", "bb", "sa")
+        for h, (a, e) in enumerate(halves):
+            vtt(T.bb[:, a:e], ["bb%d" % h], bank(4 + h, HALF), ["ps%d" % (4 + h)], T.mk[:, a:e], ["mk"], lt)
+        op("V", ["m1", "bb0", "bb1"], ["sa"], lambda: V.tensor_tensor_scan(full("sa"), full("m1"), full("bb"), 0.0, mult, add))
         vtt(off("tm"), ["tm"], ends("sa"), ["sa"], off(dz), [dz], mult)
         tiny("pw", "tm", lz, add)
         op("V", ["pw"], ["o0"], lambda: V.tensor_copy(off("o0"), off("pw")))
-        acopy(full("ssb"), ["ssb"], bank(4), ["ps4"])
+        for h, (a, e) in enumerate(halves):
+            acopy(T.ssb[:, a:e], ["ssb%d" % h], bank(4 + h, HALF), ["ps%d" % (4 + h)])
 
         agather("ic", "o0", "t0")
         agather("t0", "o0", "t1")
@@ -267,15 +282,22 @@ def rank_program(g, core, T, topo):
         low("ic", "o0", "ic2", "l0")
         low("l0", "o0", "ic", "l1")
         tiny("cp", "cw", "pw", sub)
-        op("V", ["ps4"], ["ssc"], lambda: V.tensor_copy(full("ssc"), bank(4)))
+        vts("pq", "pw", 0.25, None, add)
+        op("V", ["cp", "sc1"], ["cs"], lambda: V.tensor_scalar(off("cs"), off("cp"), T.sc1[:, 0:1], None, mult))
+        for h, (a, e) in enumerate(halves):
+            op("V", ["ps%d" % (4 + h)], ["ssc%d" % h], lambda: V.tensor_copy(T.ssc[:, a:e], bank(4 + h, HALF)))
+        again("l1", "k1")
         for j in range(1, 7):
             sn = "sa" if j % 2 else "sb"
             scan("dw", "t%d" % (j + 1), sn)
             offsets(sn, "o%d" % j)
             if j < 6:
                 agather("t%d" % (j + 1), "o%d" % j, "t%d" % (j + 2))
-            again("l%d" % j, "k%d" % j)
             low("l%d" % j, "o%d" % j, "k%d" % j, "l%d" % (j + 1))
+            if k == 0 and j < 5:
+                units("e8", "c8", [j - 1])
+            if j < 6:
+                acopy(full("k%d" % (j + 1)), ["k%d" % (j + 1)], full("l%d" % (j + 1)), ["l%d" % (j + 1)])
         low("l7", "o6", "k6", "l8")
 
         for b in range(4):
@@ -283,10 +305,10 @@ def rank_program(g, core, T, topo):
         for b in range(3):
             acopy(pl("z0", b), ["z0%d" % b], bank(4 + b), ["ps%d" % (4 + b)])
 
-        vtt(full("fl"), ["fl"], full("l8").indirect(off("o0")), ["l8", "o0"], full("im"), ["im"], eq)
-        scan("m1", "fl", "sa")
-        vtt(off("tn"), ["tn"], ends("sa"), ["sa"], off("cp"), ["cp"], mult)
-        tiny("tw", "tn", "pw", add)
+        vtt(full("fl"), ["fl"], full("l8").indirect(off("o0")), ["l8", "o0"], full("ic"), ["ic"], eq)
+        scan("dw", "fl", "sa")
+        vtt(off("tn"), ["tn"], ends("sa"), ["sa"], off("cs"), ["cs"], mult)
+        tiny("tw", "tn", "pq", add)
         op("V", ["tw"], [pt], lambda: V.tensor_copy(off(pt), off("tw")))
         send(dst, "ra%d" % k, [pt], off(ta), off(pt))
         agather("l8", "o6", "rb")
@@ -294,6 +316,9 @@ def rank_program(g, core, T, topo):
 
         def vcast0(b):
             op("V", ["ps%d" % (4 + b)], ["d0%d" % b], lambda: V.tensor_copy(pl("zd", b), bank(4 + b)))
+
+        def fcast(b):
+            acopy(pl("fo", b), ["fo%d" % b], bank(b), ["ps%d" % b])
 
         agather("ic", pt, "q0")
         agather("q0", pt, "q1")
@@ -304,14 +329,22 @@ def rank_program(g, core, T, topo):
         offsets("sb", pu)
         send(dst, "rb%d" % k, [pu], off(tb), off(pu))
         vcast0(1)
+        if k:
+            fcast(0)
         agather("q1", pu, "q2")
+        if k:
+            fcast(1)
+            fcast(2)
         scan("dw", "rd", "sa")
         offsets("sa", "orr")
-        vtt(full("cm"), ["cm"], full("ssb").indirect(off("orr")), ["ssb", "orr"], full("ssc"), ["ssc"], gt)
         scan("dw", "q2", "sb")
         offsets("sb", pv)
         send(dst, "rd%d" % k, [pv], off(td), off(pv))
+        vtt(full("cm"), ["cm"], full("ssb").indirect(off("orr")), ["ssb0", "ssb1", "orr"], full("ssc"), ["ssc0", "ssc1"], gt)
         scan("dw", "cm", "sa")
+        if k == 0:
+            units("e1", "c1")
+            own()
 
         def step(i, b, o):
             x, out = "z%d" % (i - 1), (el("z3", b) if i == 3 else pl("z%d" % i, b))
@@ -345,60 +378,69 @@ def rank_program(g, core, T, topo):
         for b in (2, 3):
             acopy(pl("gb", b - 2), ["gb%d" % b], pl("z0", b).indirect(off(ta)), ["z0%d" % b, ta])
         step(1, 0, ta)
-        twin(1, 0)
+        op("V", ["sa", "sc1"], ["xm"], lambda: V.tensor_scalar(off("xm"), ends("sa"), T.sc1[:, 0:1], 0.5, mult, gt))
         half(2)
         stage(2, 2, tb)
+        twin(1, 0)
         step(1, 1, ta)
-        twin(1, 1)
+        tiny("xd", "xm", dz, mult)
         half(3)
         stage(2, 3, tb)
+        twin(1, 1)
         step(2, 0, tb)
-        twin(2, 0)
+        vts("xe", "xm", -2.0, 1.0, mult, add)
         pairs(2, 2)
+        twin(2, 0)
         op("V", [td], ["te"], lambda: V.tensor_scalar(off("te"), off(td), 2.0, 1.0, mult, add))
         stage(3, 2, "te")
         step(2, 1, tb)
-        twin(2, 1)
+        tiny(lz1, lz, "xd", add)
         pairs(2, 3)
         stage(3, 3, "te")
-        for b in range(3):
-            acopy(pl("fo", b), ["fo%d" % b], bank(b), ["ps%d" % b])
-        pairs(3, 2)
-        step(3, 0, td)
-        pairs(3, 3)
-        step(3, 1, td)
-        quant("z3", ["z30", "z31", "z32", "z33"], zq, zs)
-
         if k == 0:
-            quant("vt", ["vt"], "vq", "vqs", 128)
-        op("V", ["sa", "sc1"], ["xm"], lambda: V.tensor_scalar(off("xm"), ends("sa"), T.sc1[:, 0:1], 0.5, mult, gt))
-        tiny("xd", "xm", dz, mult)
-        vts("xe", "xm", -2.0, 1.0, mult, add)
-        tiny(lz1, lz, "xd", add)
+            for b in range(3):
+                fcast(b)
+        twin(2, 1)
+        pairs(3, 2)
         tiny(dz1, dz, "xe", mult)
         if last:
-            tiny("l1f", lz1, dz1, add)
             op("V", [lz1], ["loa"], lambda: V.tensor_copy(T.lo[:, 0:K], off(lz1)))
+        step(3, 0, td)
+        if last:
+            tiny("l1f", lz1, dz1, add)
+        pairs(3, 3)
+        if k == 0:
+            quant("vt", ["vt"], "vq", "vqs", 128)
+        if last:
             op("V", ["l1f"], ["lob"], lambda: V.tensor_copy(T.lo[:, K:2 * K], off("l1f")))
+        step(3, 1, td)
+        zk = parts(zq)
+        for h in (0, 1):
+            quant_half("z3", ["z30", "z31", "z32", "z33"], zq, zs, h)
+            mm(h, "wq", 0, ["wqc", "wqp"], zq, zs, [zk[h]], *halves[h])
+        if last:
+            acopy(T.lrep[:], ["lrep"], full("fi").indirect(T.lo[:, 0:2 * K]), ["fi", "loa", "lob"])
+            dma("Y", "dls", ["lrep"], [], T.ls[:], T.lrep[0:128:16, :])
 
-        for b in range(4):
-            mm(4 + b, "wq", 128 * b, ["wqc", "wqp"], zq, zs, [zq])
-        for b in range(4):
+        for b in range(1, 4):
+            mm(4 + b, "wq", 128 * b, ["wqc", "wqp"], zq, zs, zk)
+        op("V", ["ps0"], ["hb0a"], lambda: V.tensor_scalar(T.hb[:, 0:HALF], bank(0, HALF), 0.03125, None, mult))
+        acopy(T.hb[:, HALF:C], ["hb0b"], bank(1, HALF), ["ps1"], 0.03125)
+        for b in range(1, 4):
             acopy(pl("hb", b), ["hb%d" % b], bank(4 + b), ["ps%d" % (4 + b)], 0.03125)
         acopy(full("xg"), ["xg"], pl("hb", 3).indirect(off(pt)), ["hb3", pt])
         for b in range(3):
-            vtt(el(nx, b), [nx], pl("hb", b).indirect(off(pt)), ["hb%d" % b, pt], pl("fo", b), ["fo%d" % b], add)
-        vtt(el(nx, 3), [nx], full("xg"), ["xg"], bank(3), ["ps3"], add)
+            vtt(el(nx, b), [nx + "_%d" % b], pl("hb", b).indirect(off(pt)), ([] if b else ["hb0a", "hb0b"]) + ["hb%d" % b, pt], pl("fo", b), ["fo%d" % b], add)
+        vtt(el(nx, 3), [nx + "_3"], full("xg"), ["xg"], bank(3), ["ps3"], add)
 
-    acopy(T.lrep[:], ["lrep"], full("fi").indirect(T.lo[:, 0:2 * K]), ["fi", "loa", "lob"])
-    dma("Y", "dls", ["lrep"], [], T.ls[:], T.lrep[0:128:16, :])
     xq, xs = "xq%d" % ROUNDS, "xs%d" % ROUNDS
-    quant("xt%d" % ROUNDS, ["xt%d" % ROUNDS], xq, xs)
-    mm(0, "vq", 0, ["vq"], xq, xs, [xq], 0, HALF)
-    mm(1, "vq", 0, ["vq"], xq, xs, [xq], HALF, C)
-    dma("Y", "doc", [xq], [], T.oc[:], full(xq).bitcast(dt.uint8))
+    xk = parts(xq)
+    for h in (0, 1):
+        quant_half("xt%d" % ROUNDS, ["xt%d_%d" % (ROUNDS, b) for b in range(4)], xq, xs, h)
+        mm(h, "vq", 0, ["vq"], xq, xs, [xk[h]], *halves[h])
+    dma("Y", "doc", xk, [], T.oc[:], full(xq).bitcast(dt.uint8))
     for i in range(4):
-        dma("Y", "dsc%d" % i, [xq], [], T.osc[4 * i:4 * i + 4, :], T[xs][32 * i:32 * i + 4, :])
+        dma("Y", "dsc%d" % i, xk, [], T.osc[4 * i:4 * i + 4, :], T[xs][32 * i:32 * i + 4, :])
     acopy(T.yo[:, 0:HALF], ["yo0"], bank(0, HALF), ["ps0"])
     op("V", ["ps1"], ["yo1"], lambda: V.tensor_copy(T.yo[:, HALF:C], bank(1, HALF)))
     dma("A", "dy0", ["yo0"], [], T.y[:, 0:HALF], T.yo[:, 0:HALF])

@@ -5,6 +5,7 @@ K = C // 16
 STEP = [4, 1, 2]
 ROUNDS = len(STEP)
 HALF = C // 2
+CUT = 160
 
 SCRATCH = {}
 
@@ -23,7 +24,7 @@ def _declare():
         s["zq%d" % k] = ("sbuf", [128, C], "float8_e4m3fn_x4")
         s["zs%d" % k] = ("sbuf", [128, C], "uint8")
     for n, w in (("ut", 512), ("vt", 512), ("em", 520), ("en", 520), ("e1", 520), ("e8", 520), ("ic", C), ("m1", C), ("mk", C),
-                 ("dw", C), ("bb", C), ("sa", C), ("sb", C), ("fl", C), ("cm", C), ("rb", C), ("rc", C), ("rd", C),
+                 ("dw", C), ("bb", C), ("sa", C), ("sb", C), ("sc", C), ("sd", C), ("se", C), ("fl", C), ("cm", C), ("rb", C), ("rc", C), ("rd", C),
                  ("q0", C), ("q1", C), ("q2", C), ("xg", C), ("alt", 2 * C), ("st", 12 * C), ("tab", 24 * C), ("ic2", C), ("zd", 6 * C),
                  ("fo", 4 * C), ("z0", 4 * C), ("z1", 4 * C), ("z2", 4 * C), ("z3", 4 * C), ("gb", 2 * C), ("hb", 4 * C)):
         s[n] = ("sbuf", [128, w], "bfloat16")
@@ -119,17 +120,27 @@ def rank_program(g, core, T, topo):
     tables = {n: i * C for i, n in enumerate(["t%d" % i for i in range(9)] + ["l%d" % i for i in range(9)] + ["k%d" % i for i in range(1, 7)])}
     lists = {n: i * 32 for i, n in enumerate(["lz%d" % i for i in range(ROUNDS + 1)] + ["dz%d" % i for i in range(ROUNDS + 1)])}
 
-    def full(n):
+    halves = ((0, CUT), (CUT, C))
+    wide = (CUT, C - CUT)
+
+    def parts(n):
+        return [n + "a", n + "b"]
+
+    def full(n, h=None):
+        a, e = (0, C) if h is None else halves[h]
         if n in tables:
-            return T.tab[:, tables[n]:tables[n] + C]
-        return T[n][:, 0:C]
+            return T.tab[:, tables[n] + a:tables[n] + e]
+        return T[n][:, a:e]
 
     picks = {n: i * 32 for i, n in enumerate(["o%d" % i for i in range(7)] + ["orr", "te"])}
     sent = {n + str(i): (3 * i + j) * 32 for i in range(ROUNDS) for j, n in enumerate(["pt", "pu", "pv"])}
 
-    def off(n):
+    def off(n, h=None):
         if n in picks:
-            return T.ol[:, picks[n]:picks[n] + K]
+            a, e = (0, K) if h is None else (halves[h][0] // 16, halves[h][1] // 16)
+            return T.ol[:, picks[n] + a:picks[n] + e]
+        if h is not None:
+            return T[n][:, halves[h][0] // 16:halves[h][1] // 16]
         if n in sent:
             return T.snt[:, sent[n]:sent[n] + K]
         if n in lists:
@@ -142,8 +153,9 @@ def rank_program(g, core, T, topo):
     def el(n, b):
         return T[n][:, b:4 * C:4]
 
-    def ends(n):
-        return T[n][:, 15:C:16]
+    def ends(n, h=None):
+        a, e = (0, C) if h is None else halves[h]
+        return T[n][:, a + 15:e:16]
 
     def bank(i, w=C):
         return T["ps%d" % i][:, 0:w]
@@ -181,10 +193,8 @@ def rank_program(g, core, T, topo):
     def quant(t, tk, q, s, w=C):
         op("V", tk, [q], lambda: V.quantize_mx(T[q][:, 0:w], T[s][:, 0:w], T[t][:, 0:4 * w]))
 
-    halves = ((0, HALF), (HALF, C))
-
-    def parts(n):
-        return [n + "a", n + "b"]
+    def scan_part(d0, src, sk, out, h):
+        op("V", [d0] + sk, [parts(out)[h]], lambda: V.tensor_tensor_scan(full(out, h), full(d0, h), full(src, h), 0.0, mult, add))
 
     def quant_half(t, tk, q, s, h):
         a, e = halves[h]
@@ -232,6 +242,7 @@ def rank_program(g, core, T, topo):
     op("A", ["uq", "uo"], ["uq2p"], lambda: A.activation(T.uq2s[:, 0:128], T.uqs[:, 0:128].indirect(T.uo[:, 0:8]), copy))
     op("V", ["la32"], ["lz0"], lambda: V.tensor_copy(off("lz0"), off("la32")))
     tiny("dz0", "lb32", "la32", sub)
+    units("e8", "c8", [0])
 
     for k in range(ROUNDS):
         dst, src = T.cores[(rank + STEP[k]) % 8], T.cores[(rank - STEP[k]) % 8]
@@ -251,7 +262,7 @@ def rank_program(g, core, T, topo):
                 mm(b, "c1", 128 * b, ["c1%d" % b], xq, xs, xk)
 
         for h in (0, 1):
-            quant_half(xt, [xt] + [xt + "_%d" % b for b in range(4)], xq, xs, h)
+            quant_half(xt, [xt] + [xt + "_%d" % b for b in range(4 + h)], xq, xs, h)
             mm(4 + h, "uq2", 0, ["uq2c", "uq2p"], xq, xs, [xk[h]], *halves[h])
         send(dst, "rx%d" % k, xk, full(aq).bitcast(dt.uint8), full(xq).bitcast(dt.uint8))
         send(dst, "rx%d" % k, xk, full(asc), full(xs))
@@ -267,38 +278,49 @@ def rank_program(g, core, T, topo):
             dma("Y", "dws", [], ["wqp"], T.wqs[:], T.ws[:])
             dma("Y", "dv", [], ["vt"], T.vt[:], T.v[:])
 
-        for h, (a, e) in enumerate(halves):
-            vtt(T.bb[:, a:e], ["bb%d" % h], bank(4 + h, HALF), ["ps%d" % (4 + h)], T.mk[:, a:e], ["mk"], lt)
-        op("V", ["m1", "bb0", "bb1"], ["sa"], lambda: V.tensor_tensor_scan(full("sa"), full("m1"), full("bb"), 0.0, mult, add))
-        vtt(off("tm"), ["tm"], ends("sa"), ["sa"], off(dz), [dz], mult)
+        if k == 0:
+            units("e8", "c8", [1])
+        for h in (0, 1):
+            vtt(full("bb", h), ["bb%d" % h], bank(4 + h, wide[h]), ["ps%d" % (4 + h)], full("mk", h), ["mk"], lt)
+        for h in (0, 1):
+            scan_part("m1", "bb", ["bb%d" % h], "se", h)
+        vtt(off("tm"), ["tm"], ends("se"), parts("se") + [], off(dz), [dz], mult)
         tiny("pw", "tm", lz, add)
         op("V", ["pw"], ["o0"], lambda: V.tensor_copy(off("o0"), off("pw")))
-        for h, (a, e) in enumerate(halves):
-            acopy(T.ssb[:, a:e], ["ssb%d" % h], bank(4 + h, HALF), ["ps%d" % (4 + h)])
+        for h in (0, 1):
+            acopy(full("ssb", h), ["ssb%d" % h], bank(4 + h, wide[h]), ["ps%d" % (4 + h)])
 
-        agather("ic", "o0", "t0")
-        agather("t0", "o0", "t1")
+        op("V", ["ic", "o0"], ["t0b"], lambda: V.tensor_copy(full("t0", 1), full("ic").indirect(off("o0", 1))))
+        acopy(full("t0", 0), ["t0a"], full("ic").indirect(off("o0", 0)), ["ic", "o0"])
+        acopy(full("t1"), ["t1"], full("t0").indirect(off("o0")), ["t0a", "t0b", "o0"])
         agather("t1", "o0", "t2")
         low("ic", "o0", "ic2", "l0")
         low("l0", "o0", "ic", "l1")
-        tiny("cp", "cw", "pw", sub)
-        vts("pq", "pw", 0.25, None, add)
-        op("V", ["cp", "sc1"], ["cs"], lambda: V.tensor_scalar(off("cs"), off("cp"), T.sc1[:, 0:1], None, mult))
-        for h, (a, e) in enumerate(halves):
-            op("V", ["ps%d" % (4 + h)], ["ssc%d" % h], lambda: V.tensor_copy(T.ssc[:, a:e], bank(4 + h, HALF)))
-        again("l1", "k1")
+        for h in (0, 1):
+            op("V", ["ps%d" % (4 + h)], ["ssc%d" % h], lambda: V.tensor_copy(full("ssc", h), bank(4 + h, wide[h])))
+        acopy(full("k1"), ["k1"], full("l1"), ["l1"])
         for j in range(1, 7):
-            sn = "sa" if j % 2 else "sb"
-            scan("dw", "t%d" % (j + 1), sn)
-            offsets(sn, "o%d" % j)
+            sn, o, t, l, m, kj, kn = "sc" if j % 2 else "sd", "o%d" % j, "t%d" % (j + 1), "l%d" % j, "l%d" % (j + 1), "k%d" % j, "k%d" % (j + 1)
+            tk, lk, kk = [(parts(n) if j > 1 else [n, n]) for n in (t, l, kj)]
+            for h in (0, 1):
+                scan_part("dw", t, [tk[h]], sn, h)
+            for h in (0, 1):
+                op("V", [parts(sn)[h], "sc1"], [parts(o)[h]], lambda: V.tensor_scalar(off(o, h), ends(sn, h), T.sc1[:, 0:1], 144.25, mult, add))
             if j < 6:
-                agather("t%d" % (j + 1), "o%d" % j, "t%d" % (j + 2))
-            low("l%d" % j, "o%d" % j, "k%d" % j, "l%d" % (j + 1))
-            if k == 0 and j < 5:
-                units("e8", "c8", [j - 1])
+                for h in (0, 1):
+                    nt = "t%d" % (j + 2)
+                    acopy(full(nt, h), [parts(nt)[h]], full(t).indirect(off(o, h)), tk + [parts(o)[h]])
+            for h in (0, 1):
+                vtt(full(m, h), [parts(m)[h]], full(l).indirect(off(o, h)), lk + [parts(o)[h]], full(kj, h), [kk[h]], amin)
             if j < 6:
-                acopy(full("k%d" % (j + 1)), ["k%d" % (j + 1)], full("l%d" % (j + 1)), ["l%d" % (j + 1)])
-        low("l7", "o6", "k6", "l8")
+                for h in (0, 1):
+                    acopy(full(kn, h), [parts(kn)[h]], full(m, h), [parts(m)[h]])
+            if k == 0 and j in (2, 3):
+                units("e8", "c8", [j])
+        o6k = parts("o6")
+        tiny("cp", "cw", "pw", sub)
+        vtt(full("l8"), ["l8"], full("l7").indirect(off("o6")), parts("l7") + o6k, full("k6"), parts("k6"), amin)
+        op("V", ["cp", "sc1"], ["cs"], lambda: V.tensor_scalar(off("cs"), off("cp"), T.sc1[:, 0:1], None, mult))
 
         for b in range(4):
             mm(4 + b, "c8", 128 * b, ["c8%d" % b], aq, asc, [aq])
@@ -306,12 +328,13 @@ def rank_program(g, core, T, topo):
             acopy(pl("z0", b), ["z0%d" % b], bank(4 + b), ["ps%d" % (4 + b)])
 
         vtt(full("fl"), ["fl"], full("l8").indirect(off("o0")), ["l8", "o0"], full("ic"), ["ic"], eq)
+        vts("pq", "pw", 0.25, None, add)
         scan("dw", "fl", "sa")
         vtt(off("tn"), ["tn"], ends("sa"), ["sa"], off("cs"), ["cs"], mult)
         tiny("tw", "tn", "pq", add)
         op("V", ["tw"], [pt], lambda: V.tensor_copy(off(pt), off("tw")))
         send(dst, "ra%d" % k, [pt], off(ta), off(pt))
-        agather("l8", "o6", "rb")
+        acopy(full("rb"), ["rb"], full("l8").indirect(off("o6")), ["l8"] + o6k)
         acopy(pl("z0", 3), ["z03"], bank(7), ["ps7"])
 
         def vcast0(b):
@@ -322,8 +345,8 @@ def rank_program(g, core, T, topo):
 
         agather("ic", pt, "q0")
         agather("q0", pt, "q1")
-        vgather("rb", "o6", "rc")
-        vgather("rc", "o6", "rd")
+        for w, r in (("rb", "rc"), ("rc", "rd")):
+            op("V", [w] + o6k, [r], lambda: V.tensor_copy(full(r), full(w).indirect(off("o6"))))
         vcast0(0)
         scan("dw", "q1", "sb")
         offsets("sb", pu)
@@ -342,6 +365,7 @@ def rank_program(g, core, T, topo):
         send(dst, "rd%d" % k, [pv], off(td), off(pv))
         vtt(full("cm"), ["cm"], full("ssb").indirect(off("orr")), ["ssb0", "ssb1", "orr"], full("ssc"), ["ssc0", "ssc1"], gt)
         scan("dw", "cm", "sa")
+        op("V", ["sa", "sc1"], ["xm"], lambda: V.tensor_scalar(off("xm"), ends("sa"), T.sc1[:, 0:1], 0.5, mult, gt))
         if k == 0:
             units("e1", "c1")
             own()
@@ -378,23 +402,20 @@ def rank_program(g, core, T, topo):
         for b in (2, 3):
             acopy(pl("gb", b - 2), ["gb%d" % b], pl("z0", b).indirect(off(ta)), ["z0%d" % b, ta])
         step(1, 0, ta)
-        op("V", ["sa", "sc1"], ["xm"], lambda: V.tensor_scalar(off("xm"), ends("sa"), T.sc1[:, 0:1], 0.5, mult, gt))
+        tiny("xd", "xm", dz, mult)
         half(2)
         stage(2, 2, tb)
         twin(1, 0)
         step(1, 1, ta)
-        tiny("xd", "xm", dz, mult)
         half(3)
         stage(2, 3, tb)
         twin(1, 1)
         step(2, 0, tb)
-        vts("xe", "xm", -2.0, 1.0, mult, add)
         pairs(2, 2)
         twin(2, 0)
         op("V", [td], ["te"], lambda: V.tensor_scalar(off("te"), off(td), 2.0, 1.0, mult, add))
         stage(3, 2, "te")
         step(2, 1, tb)
-        tiny(lz1, lz, "xd", add)
         pairs(2, 3)
         stage(3, 3, "te")
         if k == 0:
@@ -402,49 +423,52 @@ def rank_program(g, core, T, topo):
                 fcast(b)
         twin(2, 1)
         pairs(3, 2)
-        tiny(dz1, dz, "xe", mult)
-        if last:
-            op("V", [lz1], ["loa"], lambda: V.tensor_copy(T.lo[:, 0:K], off(lz1)))
+        vts("xe", "xm", -2.0, 1.0, mult, add)
         step(3, 0, td)
-        if last:
-            tiny("l1f", lz1, dz1, add)
         pairs(3, 3)
         if k == 0:
             quant("vt", ["vt"], "vq", "vqs", 128)
-        if last:
-            op("V", ["l1f"], ["lob"], lambda: V.tensor_copy(T.lo[:, K:2 * K], off("l1f")))
-        step(3, 1, td)
+        for h, (a, e) in enumerate(halves):
+            vtt(T.z3[:, 4 * a + 1:4 * e:4], ["z31" + "ab"[h]], pl("z2", 1).indirect(off(td, h)), ["z21", "z31", td], T.zd[:, 5 * C + a:5 * C + e], ["d21"], add)
         zk = parts(zq)
         for h in (0, 1):
-            quant_half("z3", ["z30", "z31", "z32", "z33"], zq, zs, h)
+            quant_half("z3", ["z30", "z31", "z32", "z33"] + parts("z31")[0:h + 1], zq, zs, h)
             mm(h, "wq", 0, ["wqc", "wqp"], zq, zs, [zk[h]], *halves[h])
-        if last:
-            acopy(T.lrep[:], ["lrep"], full("fi").indirect(T.lo[:, 0:2 * K]), ["fi", "loa", "lob"])
-            dma("Y", "dls", ["lrep"], [], T.ls[:], T.lrep[0:128:16, :])
 
-        for b in range(1, 4):
+        tiny(lz1, lz, "xd", add)
+        tiny(dz1, dz, "xe", mult)
+        if last:
+            op("V", [lz1], ["loa"], lambda: V.tensor_copy(T.lo[:, 0:K], off(lz1)))
+            tiny("l1f", lz1, dz1, add)
+            op("V", ["l1f"], ["lob"], lambda: V.tensor_copy(T.lo[:, K:2 * K], off("l1f")))
+
+        for b in (1, 3, 2):
             mm(4 + b, "wq", 128 * b, ["wqc", "wqp"], zq, zs, zk)
-        op("V", ["ps0"], ["hb0a"], lambda: V.tensor_scalar(T.hb[:, 0:HALF], bank(0, HALF), 0.03125, None, mult))
-        acopy(T.hb[:, HALF:C], ["hb0b"], bank(1, HALF), ["ps1"], 0.03125)
-        for b in range(1, 4):
+        op("V", ["ps0"], ["hb0a"], lambda: V.tensor_scalar(T.hb[:, 0:CUT], bank(0, CUT), 0.03125, None, mult))
+        acopy(T.hb[:, CUT:C], ["hb0b"], bank(1, C - CUT), ["ps1"], 0.03125)
+        for b in (1, 3, 2):
             acopy(pl("hb", b), ["hb%d" % b], bank(4 + b), ["ps%d" % (4 + b)], 0.03125)
         acopy(full("xg"), ["xg"], pl("hb", 3).indirect(off(pt)), ["hb3", pt])
         for b in range(3):
             vtt(el(nx, b), [nx + "_%d" % b], pl("hb", b).indirect(off(pt)), ([] if b else ["hb0a", "hb0b"]) + ["hb%d" % b, pt], pl("fo", b), ["fo%d" % b], add)
-        vtt(el(nx, 3), [nx + "_3"], full("xg"), ["xg"], bank(3), ["ps3"], add)
+        for h, (a, e) in enumerate(halves):
+            vtt(T[nx][:, 4 * a + 3:4 * e:4], [nx + "_%d" % (3 + h)], T.xg[:, a:e], ["xg"], T.ps3[:, a:e], ["ps3"], add)
+        if last:
+            acopy(T.lrep[:], ["lrep"], full("fi").indirect(T.lo[:, 0:2 * K]), ["fi", "loa", "lob"])
+            dma("Y", "dls", ["lrep"], [], T.ls[:], T.lrep[0:128:16, :])
 
     xq, xs = "xq%d" % ROUNDS, "xs%d" % ROUNDS
     xk = parts(xq)
     for h in (0, 1):
-        quant_half("xt%d" % ROUNDS, ["xt%d_%d" % (ROUNDS, b) for b in range(4)], xq, xs, h)
+        quant_half("xt%d" % ROUNDS, ["xt%d_%d" % (ROUNDS, b) for b in range(4 + h)], xq, xs, h)
         mm(h, "vq", 0, ["vq"], xq, xs, [xk[h]], *halves[h])
     dma("Y", "doc", xk, [], T.oc[:], full(xq).bitcast(dt.uint8))
     for i in range(4):
         dma("Y", "dsc%d" % i, xk, [], T.osc[4 * i:4 * i + 4, :], T[xs][32 * i:32 * i + 4, :])
-    acopy(T.yo[:, 0:HALF], ["yo0"], bank(0, HALF), ["ps0"])
-    op("V", ["ps1"], ["yo1"], lambda: V.tensor_copy(T.yo[:, HALF:C], bank(1, HALF)))
-    dma("A", "dy0", ["yo0"], [], T.y[:, 0:HALF], T.yo[:, 0:HALF])
-    dma("Y", "dy1", ["yo1"], [], T.y[:, HALF:C], T.yo[:, HALF:C])
+    acopy(T.yo[:, 0:CUT], ["yo0"], bank(0, CUT), ["ps0"])
+    op("V", ["ps1"], ["yo1"], lambda: V.tensor_copy(T.yo[:, CUT:C], bank(1, C - CUT)))
+    dma("A", "dy0", ["yo0"], [], T.y[:, 0:CUT], T.yo[:, 0:CUT])
+    dma("Y", "dy1", ["yo1"], [], T.y[:, CUT:C], T.yo[:, CUT:C])
     for s in total:
         if known["Y"].get(s, 0) < total[s]:
             Q["Y"].wait_ge(T.sem[s], total[s])

from concourse.mybir import dt, AluOpType, ActivationFunctionType

C = 288
K = C // 16
STEP = [4, 1, 2]
ROUNDS = len(STEP)
HALF = C // 2
CUT = 160

SCRATCH = {}


def _declare():
    s = SCRATCH
    for k in range(ROUNDS + 1):
        s["xt%d" % k] = ("sbuf", [128, 4 * C], "bfloat16")
        s["xq%d" % k] = ("sbuf", [128, C], "float8_e4m3fn_x4")
        s["xs%d" % k] = ("sbuf", [128, C], "uint8")
    for k in range(ROUNDS):
        s["aq%d" % k] = ("sbuf", [128, C], "float8_e4m3fn_x4")
        s["as%d" % k] = ("sbuf", [128, C], "uint8")
        for n in ("ta", "tb", "td"):
            s[n + str(k)] = ("sbuf", [128, 32], "uint16")
        s["zq%d" % k] = ("sbuf", [128, C], "float8_e4m3fn_x4")
        s["zs%d" % k] = ("sbuf", [128, C], "uint8")
    for n, w in (("ut", 512), ("vt", 512), ("em", 520), ("en", 520), ("e1", 520), ("e8", 520), ("ic", C), ("m1", C), ("mk", C),
                 ("dw", C), ("bb", C), ("sa", C), ("sb", C), ("sc", C), ("sd", C), ("se", C), ("fl", C), ("cm", C), ("rb", C), ("rc", C), ("rd", C),
                 ("q0", C), ("q1", C), ("q2", C), ("xg", C), ("alt", 2 * C), ("st", 12 * C), ("tab", 24 * C), ("ic2", C), ("zd", 6 * C),
                 ("fo", 4 * C), ("z0", 4 * C), ("z1", 4 * C), ("z2", 4 * C), ("z3", 4 * C), ("gb", 2 * C), ("hb", 4 * C)):
        s[n] = ("sbuf", [128, w], "bfloat16")
    for n, w in (("ol", 32 * 9), ("snt", 32 * 3 * ROUNDS), ("uo", 32)):
        s[n] = ("sbuf", [128, w], "uint16")
    s["lo"] = ("sbuf", [128, 64], "uint16")
    for n, w in (("ri", C), ("rr", C), ("pi", 8), ("pj", 8), ("k16", 24), ("uj", 8), ("la32", 24), ("lb32", 24)):
        s[n] = ("sbuf", [128, w], "int32")
    for n, w in (("wa", C), ("ssb", C), ("ssc", C), ("fi", C), ("lrep", 2 * C), ("yo", C), ("sc0", 8), ("sc1", 8), ("pf", 8), ("cw", 24), ("tm", 24), ("pw", 24),
                 ("cp", 24), ("cs", 24), ("pq", 24), ("tn", 24), ("tw", 24), ("xm", 24), ("xd", 24), ("xe", 24), ("l1f", 24), ("lst", 32 * 8)):
        s[n] = ("sbuf", [128, w], "float32")
    for n, w in (("uq", 128), ("uq2", 128), ("vq", 128), ("wq", 512), ("c1", 512), ("c8", 512)):
        s[n] = ("sbuf", [128, w], "float8_e4m3fn_x4")
        s[n + "s"] = ("sbuf", [128, w], "uint8")
    for i in range(8):
        s["ps%d" % i] = ("psum", [128, 512], "float32")


_declare()
SEMAPHORES = (["eV", "eA", "eP", "eG", "lsem"] + ["dx", "du", "dla", "dlb", "dwc", "dws", "dv", "dls", "doc", "dy0", "dy1"] + ["dsc%d" % i for i in range(4)]
              + ["%s%d" % (n, k) for n in ("rx", "ra", "rb", "rd") for k in range(ROUNDS)])


def rank_program(g, core, T, topo):
    rank = T.rank_of(core)
    if rank is None:
        return
    Q = {"V": g.vector, "A": g.scalar, "P": g.tensor, "G": g, "Y": g.sync}
    count, known, snap, lastw, readers, total = {}, {q: {} for q in Q}, {}, {}, {}, {}

    def wait_for(q, toks):
        best = {}
        for s, n in toks:
            best[s] = max(n, best.get(s, 0))
        todo = [(s, n) for s, n in best.items() if known[q].get(s, 0) < n]
        todo = [t for t in todo if not any(u != t and snap.get(u, {}).get(t[0], 0) >= t[1] for u in todo)]
        for s, n in todo:
            Q[q].wait_ge(T.sem[s], n)
            for a, b in list(snap.get((s, n), {}).items()) + [(s, n)]:
                known[q][a] = max(b, known[q].get(a, 0))

    def before(q, reads, writes):
        toks = []
        for b in reads:
            if b in lastw:
                toks.append(lastw[b])
            if b[:2] == "ps":
                toks += [t for t in readers.get(b, []) if t[0] != "e" + q]
        for b in writes:
            if b in lastw:
                toks.append(lastw[b])
            toks += readers.get(b, [])
        wait_for(q, toks)

    def after(q, tok, reads, writes):
        snap[tok] = dict(known[q])
        for b in reads:
            readers.setdefault(b, []).append(tok)
        for b in writes:
            lastw[b] = tok
            readers[b] = []

    def op(q, reads, writes, call):
        before(q, reads, writes)
        s = "e" + q
        count[s] = count.get(s, 0) + 1
        call().then_inc(T.sem[s], 1)
        total[s] = count[s]
        after(q, (s, count[s]), reads, writes)

    def dma(q, sem, reads, writes, out, in_):
        before(q, reads, writes)
        Q[q].dma_start(out, in_).then_inc(T.sem[sem], 16)
        total[sem] = 16
        after(q, (sem, 16), reads, writes)

    def send(dst, sem, reads, out, in_):
        before("G", reads, [])
        rid, pid = topo.addr(dst, core)
        g.remote_dma(out, in_, T.sem[sem], T.sem.lsem, pid, rid, topo.mask(core, dst))
        total["lsem"] = total.get("lsem", 0) + len(topo.engines(core, dst))

    def lands(src, sem, buf, writes=1):
        n = writes * len(topo.engines(src, core))
        total[sem] = n
        for b in buf:
            lastw[b] = (sem, n)
            readers[b] = []

    V, A, P = g.vector, g.scalar, g.tensor
    mult, add, sub, lt, gt, eq, amin = (AluOpType.mult, AluOpType.add, AluOpType.subtract, AluOpType.is_lt, AluOpType.is_gt, AluOpType.is_equal, AluOpType.min)
    copy = ActivationFunctionType.Copy
    tables = {n: i * C for i, n in enumerate(["t%d" % i for i in range(9)] + ["l%d" % i for i in range(9)] + ["k%d" % i for i in range(1, 7)])}
    lists = {n: i * 32 for i, n in enumerate(["lz%d" % i for i in range(ROUNDS + 1)] + ["dz%d" % i for i in range(ROUNDS + 1)])}

    halves = ((0, CUT), (CUT, C))
    wide = (CUT, C - CUT)

    def parts(n):
        return [n + "a", n + "b"]

    def full(n, h=None):
        a, e = (0, C) if h is None else halves[h]
        if n in tables:
            return T.tab[:, tables[n] + a:tables[n] + e]
        return T[n][:, a:e]

    picks = {n: i * 32 for i, n in enumerate(["o%d" % i for i in range(7)] + ["orr", "te"])}
    sent = {n + str(i): (3 * i + j) * 32 for i in range(ROUNDS) for j, n in enumerate(["pt", "pu", "pv"])}

    def off(n, h=None):
        if n in picks:
            a, e = (0, K) if h is None else (halves[h][0] // 16, halves[h][1] // 16)
            return T.ol[:, picks[n] + a:picks[n] + e]
        if h is not None:
            return T[n][:, halves[h][0] // 16:halves[h][1] // 16]
        if n in sent:
            return T.snt[:, sent[n]:sent[n] + K]
        if n in lists:
            return T.lst[:, lists[n]:lists[n] + K]
        return T[n][:, 0:K]

    def pl(n, b):
        return T[n][:, b * C:(b + 1) * C]

    def el(n, b):
        return T[n][:, b:4 * C:4]

    def ends(n, h=None):
        a, e = (0, C) if h is None else halves[h]
        return T[n][:, a + 15:e:16]

    def bank(i, w=C):
        return T["ps%d" % i][:, 0:w]

    def vtt(out, ok, a, ak, b, bk, o):
        op("V", ak + bk, ok, lambda: V.tensor_tensor(out, a, b, o))

    def vts(out, a, s1, s2, o1, *o2, w=off, extra=()):
        op("V", [a] + list(extra), [out], lambda: V.tensor_scalar(w(out), w(a), s1, s2, o1, *o2))

    def scan(d0, d1, out):
        op("V", [d0, d1], [out], lambda: V.tensor_tensor_scan(full(out), full(d0), full(d1), 0.0, mult, add))

    def offsets(sc, out):
        op("V", [sc, "sc1"], [out], lambda: V.tensor_scalar(off(out), ends(sc), T.sc1[:, 0:1], 144.25, mult, add))

    def acopy(out, ok, in_, ik, scale=1.0):
        op("A", ik, ok, lambda: A.activation(out, in_, copy, scale=scale))

    def agather(win, o, out):
        acopy(full(out), [out], full(win).indirect(off(o)), [win, o])

    def vgather(win, o, out):
        op("V", [win, o], [out], lambda: V.tensor_copy(full(out), full(win).indirect(off(o))))

    def low(win, o, other, out):
        vtt(full(out), [out], full(win).indirect(off(o)), [win, o], full(other), [other], amin)

    def again(src, out):
        op("V", [src], [out], lambda: V.tensor_copy(full(out), full(src)))

    def tiny(out, a, b, o):
        vtt(off(out), [out], off(a), [a], off(b), [b], o)

    def quant(t, tk, q, s, w=C):
        op("V", tk, [q], lambda: V.quantize_mx(T[q][:, 0:w], T[s][:, 0:w], T[t][:, 0:4 * w]))

    def scan_part(d0, src, sk, out, h):
        op("V", [d0] + sk, [parts(out)[h]], lambda: V.tensor_tensor_scan(full(out, h), full(d0, h), full(src, h), 0.0, mult, add))

    def quant_half(t, tk, q, s, h):
        a, e = halves[h]
        op("V", tk, [parts(q)[h]], lambda: V.quantize_mx(T[q][:, a:e], T[s][:, a:e], T[t][:, 4 * a:4 * e]))

    def units(e, c, which=range(4)):
        for b in which:
            op("V", [e], [c + str(b)], lambda: V.quantize_mx(T[c][:, 128 * b:128 * b + 128], T[c + "s"][:, 128 * b:128 * b + 128],
                                                             T[e][:, 4 - b:4 - b + 512]))

    def mm(i, l, a, lk, r, rs, rk, c0=0, c1=C):
        op("P", lk + rk, ["ps%d" % i], lambda: P.matmul_mx(bank(i, c1 - c0), T[l][:, a:a + 128], T[l + "s"][:, a:a + 128],
                                                           T[r][:, c0:c1], T[rs][:, c0:c1], True, True))

    def iota(out, ok, pattern, base, cm):
        op("G", [], [ok], lambda: g.iota(out, pattern, base, cm, allow_small_or_imprecise_dtypes=True))

    dma("Y", "dx", [], ["xt0"], T.xt0[:], T.x[:])
    dma("A", "du", [], ["ut"], T.ut[:], T.u[:])
    dma("Y", "dla", [], ["la32"], off("la32"), T.la[:])
    dma("A", "dlb", [], ["lb32"], off("lb32"), T.lb[:])
    op("V", [], ["em"], lambda: V.memset(T.em[:], 0.125))
    op("V", [], ["en"], lambda: V.memset(T.en[:], 1.0))
    iota(T.ri[:], "ri", [[-1, C]], C, 1)
    iota(T.pi[:, 0:1], "pi", [[0, 1]], 0, 1)
    iota(T.uj[:, 0:8], "uj", [[16, 8]], 0, 0)
    iota(off("k16"), "k16", [[16, K]], 0, 0)
    op("G", ["em"], ["e8"], lambda: g.affine_select(T.e8[:], T.em[:], [[1, 520]], eq, 0.0, -4, -4))
    iota(T.ic[:], "ic", [[1, C]], -HALF, 0)
    iota(T.ic2[:], "ic2", [[1, C]], -HALF, 0)

    vts("rr", "ri", 15, None, AluOpType.bitwise_and, w=full)
    vts("m1", "rr", 1.0, None, amin, w=full)
    vts("wa", "rr", 15.0, 65535.0, eq, mult, w=full)
    op("V", ["pi"], ["pj"], lambda: V.tensor_scalar(T.pj[:, 0:1], T.pi[:, 0:1], 15, None, AluOpType.bitwise_and))
    vts("mk", "m1", -1e29, None, mult, w=full)
    vtt(full("dw"), ["dw"], full("wa"), ["wa"], full("m1"), ["m1"], add)
    op("V", ["pj"], ["sc0"], lambda: V.tensor_scalar(T.sc0[:, 0:1], T.pj[:, 0:1], 15.0, 1.0 - 2.0 ** -16, eq, mult))
    op("V", ["pj"], ["pf"], lambda: V.tensor_copy(T.pf[:, 0:1], T.pj[:, 0:1]))
    op("V", ["uj"], ["uo"], lambda: V.tensor_copy(T.uo[:, 0:8], T.uj[:, 0:8]))
    op("V", ["sc0"], ["sc1"], lambda: V.tensor_scalar(T.sc1[:, 0:1], T.sc0[:, 0:1], 2.0 ** -16, None, add))
    vts("cw", "k16", T.pf[:, 0:1], None, add, extra=["pf"])
    quant("ut", ["ut"], "uq", "uqs", 128)
    op("V", ["uq", "uo"], ["uq2c"], lambda: V.tensor_copy(T.uq2[:, 0:128].bitcast(dt.uint32), T.uq[:, 0:128].bitcast(dt.uint32).indirect(T.uo[:, 0:8])))
    op("A", ["uq", "uo"], ["uq2p"], lambda: A.activation(T.uq2s[:, 0:128], T.uqs[:, 0:128].indirect(T.uo[:, 0:8]), copy))
    op("V", ["la32"], ["lz0"], lambda: V.tensor_copy(off("lz0"), off("la32")))
    tiny("dz0", "lb32", "la32", sub)
    units("e8", "c8", [0])

    for k in range(ROUNDS):
        dst, src = T.cores[(rank + STEP[k]) % 8], T.cores[(rank - STEP[k]) % 8]
        xt, xq, xs, aq, asc, zq, zs, lz, dz = [n + str(k) for n in ("xt", "xq", "xs", "aq", "as", "zq", "zs", "lz", "dz")]
        ta, tb, td, pt, pu, pv = [n + str(k) for n in ("ta", "tb", "td", "pt", "pu", "pv")]
        nx, lz1, dz1 = [n + str(k + 1) for n in ("xt", "lz", "dz")]
        last = k == ROUNDS - 1
        lands(src, "rx%d" % k, [aq], 2)
        lands(src, "ra%d" % k, [ta])
        lands(src, "rb%d" % k, [tb])
        lands(src, "rd%d" % k, [td])

        xk = parts(xq)

        def own():
            for b in range(4):
                mm(b, "c1", 128 * b, ["c1%d" % b], xq, xs, xk)

        for h in (0, 1):
            quant_half(xt, [xt] + [xt + "_%d" % b for b in range(4 + h)], xq, xs, h)
            mm(4 + h, "uq2", 0, ["uq2c", "uq2p"], xq, xs, [xk[h]], *halves[h])
        send(dst, "rx%d" % k, xk, full(aq).bitcast(dt.uint8), full(xq).bitcast(dt.uint8))
        send(dst, "rx%d" % k, xk, full(asc), full(xs))
        if k:
            own()
        else:
            op("G", ["en"], ["e1"], lambda: g.affine_select(T.e1[:], T.en[:], [[1, 520]], eq, 0.0, -4, -4))
            iota(T.alt[:], "alt", [[0, C], [1, 2]], 0, 0)
            iota(T.fi[:], "fi", [[1, C]], 0, 0)
        if k == 0:
            wait_for("Y", [("dx", 16)])
            dma("Y", "dwc", [], ["wqc"], T.wq[:].bitcast(dt.uint8), T.wc[:])
            dma("Y", "dws", [], ["wqp"], T.wqs[:], T.ws[:])
            dma("Y", "dv", [], ["vt"], T.vt[:], T.v[:])

        if k == 0:
            units("e8", "c8", [1])
        for h in (0, 1):
            vtt(full("bb", h), ["bb%d" % h], bank(4 + h, wide[h]), ["ps%d" % (4 + h)], full("mk", h), ["mk"], lt)
        for h in (0, 1):
            scan_part("m1", "bb", ["bb%d" % h], "se", h)
        vtt(off("tm"), ["tm"], ends("se"), parts("se") + [], off(dz), [dz], mult)
        tiny("pw", "tm", lz, add)
        op("V", ["pw"], ["o0"], lambda: V.tensor_copy(off("o0"), off("pw")))
        for h in (0, 1):
            acopy(full("ssb", h), ["ssb%d" % h], bank(4 + h, wide[h]), ["ps%d" % (4 + h)])

        op("V", ["ic", "o0"], ["t0b"], lambda: V.tensor_copy(full("t0", 1), full("ic").indirect(off("o0", 1))))
        acopy(full("t0", 0), ["t0a"], full("ic").indirect(off("o0", 0)), ["ic", "o0"])
        acopy(full("t1"), ["t1"], full("t0").indirect(off("o0")), ["t0a", "t0b", "o0"])
        agather("t1", "o0", "t2")
        low("ic", "o0", "ic2", "l0")
        low("l0", "o0", "ic", "l1")
        for h in (0, 1):
            op("V", ["ps%d" % (4 + h)], ["ssc%d" % h], lambda: V.tensor_copy(full("ssc", h), bank(4 + h, wide[h])))
        acopy(full("k1"), ["k1"], full("l1"), ["l1"])
        for j in range(1, 7):
            sn, o, t, l, m, kj, kn = "sc" if j % 2 else "sd", "o%d" % j, "t%d" % (j + 1), "l%d" % j, "l%d" % (j + 1), "k%d" % j, "k%d" % (j + 1)
            tk, lk, kk = [(parts(n) if j > 1 else [n, n]) for n in (t, l, kj)]
            for h in (0, 1):
                scan_part("dw", t, [tk[h]], sn, h)
            for h in (0, 1):
                op("V", [parts(sn)[h], "sc1"], [parts(o)[h]], lambda: V.tensor_scalar(off(o, h), ends(sn, h), T.sc1[:, 0:1], 144.25, mult, add))
            if j < 6:
                for h in (0, 1):
                    nt = "t%d" % (j + 2)
                    acopy(full(nt, h), [parts(nt)[h]], full(t).indirect(off(o, h)), tk + [parts(o)[h]])
            for h in (0, 1):
                vtt(full(m, h), [parts(m)[h]], full(l).indirect(off(o, h)), lk + [parts(o)[h]], full(kj, h), [kk[h]], amin)
            if j < 6:
                for h in (0, 1):
                    acopy(full(kn, h), [parts(kn)[h]], full(m, h), [parts(m)[h]])
            if k == 0 and j in (2, 3):
                units("e8", "c8", [j])
        o6k = parts("o6")
        tiny("cp", "cw", "pw", sub)
        vtt(full("l8"), ["l8"], full("l7").indirect(off("o6")), parts("l7") + o6k, full("k6"), parts("k6"), amin)
        op("V", ["cp", "sc1"], ["cs"], lambda: V.tensor_scalar(off("cs"), off("cp"), T.sc1[:, 0:1], None, mult))

        for b in range(4):
            mm(4 + b, "c8", 128 * b, ["c8%d" % b], aq, asc, [aq])
        for b in range(3):
            acopy(pl("z0", b), ["z0%d" % b], bank(4 + b), ["ps%d" % (4 + b)])

        vtt(full("fl"), ["fl"], full("l8").indirect(off("o0")), ["l8", "o0"], full("ic"), ["ic"], eq)
        vts("pq", "pw", 0.25, None, add)
        scan("dw", "fl", "sa")
        vtt(off("tn"), ["tn"], ends("sa"), ["sa"], off("cs"), ["cs"], mult)
        tiny("tw", "tn", "pq", add)
        op("V", ["tw"], [pt], lambda: V.tensor_copy(off(pt), off("tw")))
        send(dst, "ra%d" % k, [pt], off(ta), off(pt))
        acopy(full("rb"), ["rb"], full("l8").indirect(off("o6")), ["l8"] + o6k)
        acopy(pl("z0", 3), ["z03"], bank(7), ["ps7"])

        def vcast0(b):
            op("V", ["ps%d" % (4 + b)], ["d0%d" % b], lambda: V.tensor_copy(pl("zd", b), bank(4 + b)))

        def fcast(b):
            acopy(pl("fo", b), ["fo%d" % b], bank(b), ["ps%d" % b])

        agather("ic", pt, "q0")
        agather("q0", pt, "q1")
        for w, r in (("rb", "rc"), ("rc", "rd")):
            op("V", [w] + o6k, [r], lambda: V.tensor_copy(full(r), full(w).indirect(off("o6"))))
        vcast0(0)
        scan("dw", "q1", "sb")
        offsets("sb", pu)
        send(dst, "rb%d" % k, [pu], off(tb), off(pu))
        vcast0(1)
        if k:
            fcast(0)
        agather("q1", pu, "q2")
        if k:
            fcast(1)
            fcast(2)
        scan("dw", "rd", "sa")
        offsets("sa", "orr")
        scan("dw", "q2", "sb")
        offsets("sb", pv)
        send(dst, "rd%d" % k, [pv], off(td), off(pv))
        vtt(full("cm"), ["cm"], full("ssb").indirect(off("orr")), ["ssb0", "ssb1", "orr"], full("ssc"), ["ssc0", "ssc1"], gt)
        scan("dw", "cm", "sa")
        op("V", ["sa", "sc1"], ["xm"], lambda: V.tensor_scalar(off("xm"), ends("sa"), T.sc1[:, 0:1], 0.5, mult, gt))
        if k == 0:
            units("e1", "c1")
            own()

        def step(i, b, o):
            x, out = "z%d" % (i - 1), (el("z3", b) if i == 3 else pl("z%d" % i, b))
            n = 2 * (i - 1) + b
            vtt(out, ["z%d%d" % (i, b)], pl(x, b).indirect(off(o)), [x + str(b), o], pl("zd", n), ["d%d%d" % (i - 1, b)], add)

        def twin(i, b):
            n = 2 * i + b
            op("V", ["z%d%d" % (i, b)], ["d%d%d" % (i, b)], lambda: V.tensor_copy(pl("zd", n), pl("z%d" % i, b)))

        def stream(i, b):
            n = {1: 0, 2: 4, 3: 8}[i] + 2 * (b - 2)
            return n * C, (n + 2) * C

        def stage(i, b, o):
            a, e = stream(i, b)
            s, z = stream(1, b)
            win, one, xk = (T.st[:, s:z], T.st[:, s + 1:z:2], "u%d" % b) if i == 3 else (pl("z1", b), pl("z1", b), "z1%d" % b)
            acopy(T.st[:, a + 1:e:2], ["y%d%d" % (i, b)], one, [xk])
            acopy(T.st[:, a:e:2], ["w%d%d" % (i, b)], win.indirect(off(o)), [xk, o])

        def pairs(i, b):
            a, e = stream(i, b)
            s, z = stream(1, b)
            out, ok = (T.z3[:, b - 2:4 * C:2], ["z3%d" % b, "z3%d" % (b - 2)]) if i == 3 else (T.st[:, s:z], ["u%d" % b])
            op("V", ["alt", "y%d%d" % (i, b), "w%d%d" % (i, b)], ok, lambda: V.tensor_tensor_scan(out, T.alt[:], T.st[:, a:e], 0.0, mult, add))

        def half(b):
            vtt(pl("z1", b), ["z1%d" % b], pl("gb", b - 2), ["gb%d" % b], bank(4 + b), ["ps%d" % (4 + b)], add)

        for b in (2, 3):
            acopy(pl("gb", b - 2), ["gb%d" % b], pl("z0", b).indirect(off(ta)), ["z0%d" % b, ta])
        step(1, 0, ta)
        tiny("xd", "xm", dz, mult)
        half(2)
        stage(2, 2, tb)
        twin(1, 0)
        step(1, 1, ta)
        half(3)
        stage(2, 3, tb)
        twin(1, 1)
        step(2, 0, tb)
        pairs(2, 2)
        twin(2, 0)
        op("V", [td], ["te"], lambda: V.tensor_scalar(off("te"), off(td), 2.0, 1.0, mult, add))
        stage(3, 2, "te")
        step(2, 1, tb)
        pairs(2, 3)
        stage(3, 3, "te")
        if k == 0:
            for b in range(3):
                fcast(b)
        twin(2, 1)
        pairs(3, 2)
        vts("xe", "xm", -2.0, 1.0, mult, add)
        step(3, 0, td)
        pairs(3, 3)
        if k == 0:
            quant("vt", ["vt"], "vq", "vqs", 128)
        for h, (a, e) in enumerate(halves):
            vtt(T.z3[:, 4 * a + 1:4 * e:4], ["z31" + "ab"[h]], pl("z2", 1).indirect(off(td, h)), ["z21", "z31", td], T.zd[:, 5 * C + a:5 * C + e], ["d21"], add)
        zk = parts(zq)
        for h in (0, 1):
            quant_half("z3", ["z30", "z31", "z32", "z33"] + parts("z31")[0:h + 1], zq, zs, h)
            mm(h, "wq", 0, ["wqc", "wqp"], zq, zs, [zk[h]], *halves[h])

        tiny(lz1, lz, "xd", add)
        tiny(dz1, dz, "xe", mult)
        if last:
            op("V", [lz1], ["loa"], lambda: V.tensor_copy(T.lo[:, 0:K], off(lz1)))
            tiny("l1f", lz1, dz1, add)
            op("V", ["l1f"], ["lob"], lambda: V.tensor_copy(T.lo[:, K:2 * K], off("l1f")))

        for b in (1, 3, 2):
            mm(4 + b, "wq", 128 * b, ["wqc", "wqp"], zq, zs, zk)
        op("V", ["ps0"], ["hb0a"], lambda: V.tensor_scalar(T.hb[:, 0:CUT], bank(0, CUT), 0.03125, None, mult))
        acopy(T.hb[:, CUT:C], ["hb0b"], bank(1, C - CUT), ["ps1"], 0.03125)
        for b in (1, 3, 2):
            acopy(pl("hb", b), ["hb%d" % b], bank(4 + b), ["ps%d" % (4 + b)], 0.03125)
        acopy(full("xg"), ["xg"], pl("hb", 3).indirect(off(pt)), ["hb3", pt])
        for b in range(3):
            vtt(el(nx, b), [nx + "_%d" % b], pl("hb", b).indirect(off(pt)), ([] if b else ["hb0a", "hb0b"]) + ["hb%d" % b, pt], pl("fo", b), ["fo%d" % b], add)
        for h, (a, e) in enumerate(halves):
            vtt(T[nx][:, 4 * a + 3:4 * e:4], [nx + "_%d" % (3 + h)], T.xg[:, a:e], ["xg"], T.ps3[:, a:e], ["ps3"], add)
        if last:
            acopy(T.lrep[:], ["lrep"], full("fi").indirect(T.lo[:, 0:2 * K]), ["fi", "loa", "lob"])
            dma("Y", "dls", ["lrep"], [], T.ls[:], T.lrep[0:128:16, :])

    xq, xs = "xq%d" % ROUNDS, "xs%d" % ROUNDS
    xk = parts(xq)
    for h in (0, 1):
        quant_half("xt%d" % ROUNDS, ["xt%d_%d" % (ROUNDS, b) for b in range(4 + h)], xq, xs, h)
        mm(h, "vq", 0, ["vq"], xq, xs, [xk[h]], *halves[h])
    dma("Y", "doc", xk, [], T.oc[:], full(xq).bitcast(dt.uint8))
    for i in range(4):
        dma("Y", "dsc%d" % i, xk, [], T.osc[4 * i:4 * i + 4, :], T[xs][32 * i:32 * i + 4, :])
    acopy(T.yo[:, 0:CUT], ["yo0"], bank(0, CUT), ["ps0"])
    op("V", ["ps1"], ["yo1"], lambda: V.tensor_copy(T.yo[:, CUT:C], bank(1, C - CUT)))
    dma("A", "dy0", ["yo0"], [], T.y[:, 0:CUT], T.yo[:, 0:CUT])
    dma("Y", "dy1", ["yo1"], [], T.y[:, CUT:C], T.yo[:, CUT:C])
    for s in total:
        if known["Y"].get(s, 0) < total[s]:
            Q["Y"].wait_ge(T.sem[s], total[s])
